import numpy as np
import ml_dtypes


def mxq(x, axis, fmt="e4m3"):
    dtype, down = {"e4m3": (ml_dtypes.float8_e4m3fn, 7), "e5m2": (ml_dtypes.float8_e5m2, 14)}[fmt]
    v = np.moveaxis(np.asarray(x, np.float32).astype(ml_dtypes.bfloat16).astype(np.float64), axis, -1)
    blocks = v.reshape(v.shape[:-1] + (-1, 32))
    amax = np.abs(blocks).max(-1, keepdims=True)
    byte = np.maximum(np.where(amax > 0, np.frexp(amax)[1] - 1 + 127, 0) - down, 1)
    scale = np.exp2(byte - 127.0)
    codes = (blocks / scale).astype(np.float32).astype(dtype).astype(np.float64)
    return np.moveaxis((codes * scale).reshape(v.shape), -1, axis)


WIDE = False


def mx_kscale(k):
    if not WIDE:
        return np.ones(k)
    levels = np.array([10, -10, 5, -5, 0])
    if k % 512:
        return np.exp2(np.random.permutation(np.resize(levels, k // 32))).repeat(32)
    a = np.empty((k // 512, 16))
    for p in range(k // 512):
        a[p, :8] = np.random.permutation(np.resize(levels, 8))
        for g in range(8):
            far = levels[np.abs(levels - a[p, g]) >= 10]
            a[p, g + 8] = far[np.random.randint(len(far))]
    return np.exp2(a.ravel()).repeat(32)


def f64(x):
    return np.asarray(x).astype(np.float64)


def striped(idx):
    return np.tile(np.asarray(idx).reshape(-1, 16).T, (8, 1)).astype(np.uint16)


def unstriped(offs):
    return offs[:16].T.reshape(-1).astype(np.int64)


E2M1 = np.array([0.0, 0.5, 1.0, 1.5, 2.0, 3.0, 4.0, 6.0, -0.0, -0.5, -1.0, -1.5, -2.0, -3.0, -4.0, -6.0])


def pack_weight(w, fmt):
    k, n = w.shape
    w = f64(np.asarray(w, np.float32).astype(ml_dtypes.bfloat16)).reshape(k // 32, 32, n)
    amax = np.abs(w).max(1)
    if fmt == "e4m3":
        byte = np.frexp(amax)[1] - 1 + 127 - 7
    else:
        mant, ex = np.frexp(amax / 6.0)
        byte = np.where(mant > 0.5, ex, ex - 1) + 127
    byte = np.clip(np.where(amax > 0, byte, 1), 1, 254)
    scaled = (w * np.exp2(127.0 - byte)[:, None, :]).reshape(k, n).astype(np.float32)
    by_word = np.ascontiguousarray(scaled.reshape(k // 512, 128, 4, n).transpose(0, 1, 3, 2))
    if fmt == "e4m3":
        words = by_word.astype(ml_dtypes.float8_e4m3fn).view(np.uint8)
    else:
        c = by_word.astype(ml_dtypes.float4_e2m1fn).view(np.uint8) & 0xF
        words = (c[..., 0::2] | (c[..., 1::2] << 4)).reshape(k // 512, 128, 2 * n)
    return np.ascontiguousarray(words), np.ascontiguousarray(byte.astype(np.uint8).reshape(k // 512, 16, n))


def unpack_weight(words, scales, fmt):
    g, _, n = scales.shape
    words = np.ascontiguousarray(words).reshape(g, 128, n, -1)
    if fmt == "e4m3":
        vals = words.view(ml_dtypes.float8_e4m3fn).astype(np.float64)
    else:
        nib = np.empty((g, 128, n, 4), np.uint8)
        nib[..., 0::2] = words & 0xF
        nib[..., 1::2] = words >> 4
        vals = E2M1[nib]
    vals = vals * np.repeat(np.exp2(scales.astype(np.float64) - 127.0), 8, axis=1)[..., None]
    return vals.transpose(0, 1, 3, 2).reshape(g * 512, n)


D, T, I, Q, E, U = 512, 2048, 512, 128, 512, 512


def setup_inputs():
    n = np.random.standard_normal
    idx = np.random.permutation(T)[:I]
    idx2 = np.random.randint(0, U, I)
    fd = mx_kscale(D)
    fi = mx_kscale(I)
    ti = np.ones(T)
    ti[idx] = fi
    keysp = pack_weight(n((D, T)) / fd[:, None], "e4m3")
    return {
        "query": (n((D, Q)) * 0.4 / np.sqrt(D) * fd[:, None]).astype(np.float32),
        "keys_words": keysp[0],
        "keys_scales": keysp[1],
        "bias": (0.5 * n((Q, U))).astype(np.float32),
        "gate": (np.random.uniform(0.2, 0.8, (Q, 1))).astype(np.float32),
        "size": (np.random.uniform(0.5, 2.0, (1, I)) * fi).astype(np.float32),
        "vals": (n((E, T)) / ti).astype(np.float32),
        "offs": striped(idx),
        "offs2": striped(idx2),
    }


def reference(query, keys_words, keys_scales, bias, gate, size, vals, offs, offs2):
    idx = unstriped(offs)
    idx2 = unstriped(offs2)
    keysu = unpack_weight(keys_words, keys_scales, "e4m3")
    queryq = mxq(f64(query), 0, "e4m3")
    keysidxg = keysu[:, idx]
    a = queryq.T @ keysidxg
    s = a + f64(bias)[:, idx2]
    p = np.exp(s - np.max(s, axis=1, keepdims=True))
    r = np.exp(a - np.max(a, axis=1, keepdims=True))
    w = (f64(gate) * p / np.sum(p, axis=1, keepdims=True) + (1.0 - f64(gate)) * r / np.sum(r, axis=1, keepdims=True)) * f64(size)
    wt = w.T
    vt = f64(vals)[:, idx].T
    wtq = mxq(wt, 0, "e4m3")
    vtq = mxq(vt, 0, "e4m3")
    o = wtq.T @ vtq
    return o

@@ -1,0 +1,182 @@
+from contextlib import ExitStack
+
+import concourse.mybir as mybir
+from concourse.masks import make_identity
+
+D, T, I, Q, E, U = 512, 2048, 512, 128, 512, 512
+FLOPS = 2 * Q * I * D + 2 * Q * I * E
+
+F32 = mybir.dt.float32
+BF16 = mybir.dt.bfloat16
+I32 = mybir.dt.int32
+U32 = mybir.dt.uint32
+U16 = mybir.dt.uint16
+U8 = mybir.dt.uint8
+FP8X4 = mybir.dt.float8_e4m3fn_x4
+ALU = mybir.AluOpType
+ACT = mybir.ActivationFunctionType
+AXIS_X = mybir.AxisListType.X
+
+P = 128
+PACK = 4
+E_TILES = E // P
+
+
+def tile_attend_mixedbias_kernel(tc, query, keys_words, keys_scales, bias, gate, size, vals, offs, offs2, out):
+    nc = tc.nc
+    with ExitStack() as ctx:
+        keep = ctx.enter_context(tc.tile_pool(name="keep", bufs=1))
+        psum = ctx.enter_context(tc.psum_pool(name="psum", bufs=1))
+        turn = ctx.enter_context(tc.psum_pool(name="turn", bufs=2))
+
+        slots = keep.tile([P, I // 16], U16, name="slots")
+        buckets = keep.tile([P, I // 16], U16, name="buckets")
+        bias_pool = keep.tile([P, U], F32, name="bias_pool")
+        word_pool = keep.tile([P, T], U32, name="word_pool")
+        byte_pool = keep.tile([P, T], U8, name="byte_pool")
+        q_raw = keep.tile([P, PACK, Q], F32, name="q_raw")
+        gate_col = keep.tile([P, 1], F32, name="gate_col")
+        size_cols = keep.tile([P, PACK], F32, name="size_cols")
+        val_pool = [keep.tile([P, T], F32, name="val_pool%d" % n) for n in range(E_TILES)]
+
+        nc.gpsimd.memset(byte_pool[:].bitcast(I32), 0)
+        nc.scalar.dma_start(size_cols[:], size[0].rearrange("(p t) -> p t", t=PACK))
+        nc.scalar.dma_start(gate_col[:], gate)
+        nc.sync.dma_start(buckets[:], offs2)
+        nc.sync.dma_start(slots[:], offs)
+        nc.sync.dma_start(bias_pool[:], bias)
+        for r in range(4):
+            nc.sync.dma_start(byte_pool[r:P:32, :].bitcast(I32), keys_scales[0, r:16:4, :].bitcast(I32))
+        nc.sync.dma_start(word_pool[:].bitcast(I32), keys_words[0].rearrange("p n t -> p (n t)").bitcast(I32))
+        nc.sync.dma_start(q_raw[:], query.rearrange("(p j) q -> p j q", j=PACK))
+        for n in range(E_TILES):
+            nc.sync.dma_start(val_pool[n][:], vals[n * P : (n + 1) * P, :])
+
+        ident = keep.tile([P, P], F32, name="ident")
+        make_identity(nc, ident[:])
+
+        bias_g = keep.tile([P, I], F32, name="bias_g")
+        for h in range(2):
+            nc.vector.tensor_copy(
+                bias_g[:, h * 256 : (h + 1) * 256], bias_pool[:].indirect(buckets[:, h * 16 : (h + 1) * 16])
+            )
+        k_codes = keep.tile([P, I], U32, name="k_codes", align_bytes=64)
+        k_scales = keep.tile([P, I], U8, name="k_scales", align_bytes=64)
+        nc.vector.tensor_copy(k_scales[:], byte_pool[:].indirect(slots[:]))
+        nc.vector.tensor_copy(k_codes[:], word_pool[:].indirect(slots[:]))
+
+        q_bf = keep.tile([P, Q, PACK], BF16, name="q_bf", align_bytes=64)
+        nc.scalar.copy(q_bf[:], q_raw[:].rearrange("p j q -> p q j"))
+        q_codes = keep.tile([P, Q], U32, name="q_codes", align_bytes=64)
+        q_scales = keep.tile([P, Q], U8, name="q_scales", align_bytes=64)
+        nc.vector.quantize_mx(q_codes[:].bitcast(FP8X4), q_scales[:], q_bf[:].rearrange("p q j -> p (q j)"))
+
+        scores = psum.tile([P, I], F32, name="scores")
+        nc.tensor.matmul_mx(
+            scores[:],
+            lhsT=q_codes[:].bitcast(FP8X4),
+            lhsT_scale=q_scales[:],
+            rhs=k_codes[:].bitcast(FP8X4),
+            rhs_scale=k_scales[:],
+            start=True,
+            stop=True,
+        )
+
+        size_rows = psum.tile([P, PACK, P], F32, name="size_rows")
+        for t in range(PACK):
+            nc.tensor.transpose(size_rows[:, t, :], size_cols[:, t : t + 1].to_broadcast([P, P]), ident[:])
+        rest_col = keep.tile([P, 1], F32, name="rest_col")
+        nc.vector.tensor_scalar(rest_col[:], gate_col[:], -1.0, 1.0, ALU.mult, ALU.add)
+
+        v_codes = keep.tile([P, E], U32, name="v_codes", align_bytes=64)
+        v_scales = keep.tile([P, E], U8, name="v_scales", align_bytes=64)
+
+        def turn_pairs(rows_bf, name):
+            words = rows_bf[:].bitcast(F32)
+            turned = turn.tile([P, 2, P], F32, name="turned")
+            for u in range(2):
+                nc.tensor.transpose(turned[:, u, :], words[:, u : I // 2 : 2], ident[:])
+            grouped = keep.tile([P, P * PACK], BF16, name=name, align_bytes=64)
+            nc.scalar.copy(
+                grouped[:].bitcast(F32).rearrange("p (x u) -> p x u", u=2), turned[:].rearrange("p u x -> p x u")
+            )
+            return grouped
+
+        def gather_values(n):
+            val_g = keep.tile([P, I], BF16, name="val_g%d" % n)
+            nc.vector.tensor_copy(val_g[:], val_pool[n][:].indirect(slots[:]))
+            return turn_pairs(val_g, "val_t%d" % n)
+
+        def quantize_values(n, grouped):
+            cols = slice(n * P, (n + 1) * P)
+            nc.vector.quantize_mx(v_codes[:, cols].bitcast(FP8X4), v_scales[:, cols], grouped[:])
+
+        biased = keep.tile([P, I], F32, name="biased")
+        nc.vector.tensor_tensor(biased[:], scores[:], bias_g[:], ALU.add)
+        neg_max_r = keep.tile([P, 1], F32, name="neg_max_r")
+        neg_max_p = keep.tile([P, 1], F32, name="neg_max_p")
+        nc.vector.tensor_reduce(neg_max_r[:], scores[:], AXIS_X, ALU.max, negate=True)
+        nc.vector.tensor_reduce(neg_max_p[:], biased[:], AXIS_X, ALU.max, negate=True)
+        exp_r = keep.tile([P, I], F32, name="exp_r")
+        exp_p = keep.tile([P, I], F32, name="exp_p")
+        sum_r = keep.tile([P, 1], F32, name="sum_r")
+        sum_p = keep.tile([P, 1], F32, name="sum_p")
+        nc.scalar.activation(exp_r[:], scores[:], ACT.Exp, bias=neg_max_r[:], accum_out=sum_r[:])
+        nc.scalar.activation(exp_p[:], biased[:], ACT.Exp, bias=neg_max_p[:], accum_out=sum_p[:])
+
+        val_t0 = gather_values(0)
+
+        inv_r = keep.tile([P, 1], F32, name="inv_r")
+        inv_p = keep.tile([P, 1], F32, name="inv_p")
+        mix_r = keep.tile([P, 1], F32, name="mix_r")
+        mix_p = keep.tile([P, 1], F32, name="mix_p")
+        nc.vector.reciprocal(inv_r[:], sum_r[:])
+        nc.vector.reciprocal(inv_p[:], sum_p[:])
+        nc.vector.tensor_tensor(mix_r[:], inv_r[:], rest_col[:], ALU.mult)
+        nc.vector.tensor_tensor(mix_p[:], inv_p[:], gate_col[:], ALU.mult)
+        part_r = keep.tile([P, I], F32, name="part_r")
+        nc.scalar.activation(part_r[:], exp_r[:], ACT.Copy, scale=mix_r[:])
+
+        val_t1 = gather_values(1)
+        quantize_values(0, val_t0)
+
+        mixed = keep.tile([P, I], F32, name="mixed")
+        nc.vector.scalar_tensor_tensor(mixed[:], exp_p[:], mix_p[:], part_r[:], ALU.mult, ALU.add)
+        w_bf = keep.tile([P, I], BF16, name="w_bf")
+        nc.vector.tensor_tensor(
+            w_bf[:].rearrange("p (n t) -> p n t", t=PACK),
+            size_rows[:].rearrange("p t n -> p n t"),
+            mixed[:].rearrange("p (n t) -> p n t", t=PACK),
+            ALU.mult,
+        )
+        w_t = turn_pairs(w_bf, "w_t")
+        quantize_values(1, val_t1)
+        val_t2 = gather_values(2)
+        w_codes = keep.tile([P, Q], U32, name="w_codes", align_bytes=64)
+        w_scales = keep.tile([P, Q], U8, name="w_scales", align_bytes=64)
+        nc.vector.quantize_mx(w_codes[:].bitcast(FP8X4), w_scales[:], w_t[:])
+        quantize_values(2, val_t2)
+
+        def product(acc, first, last, name):
+            base = first * P
+            for lo, hi in ((c, min(c + 2, last)) for c in range(first, last, 2)):
+                cols = slice(lo * P, hi * P)
+                nc.tensor.matmul_mx(
+                    acc[:, lo * P - base : hi * P - base],
+                    lhsT=w_codes[:].bitcast(FP8X4),
+                    lhsT_scale=w_scales[:],
+                    rhs=v_codes[:, cols].bitcast(FP8X4),
+                    rhs_scale=v_scales[:, cols],
+                    start=True,
+                    stop=True,
+                )
+            result = keep.tile([P, (last - first) * P], F32, name=name)
+            nc.scalar.copy(result[:], acc[:])
+            nc.sync.dma_start(out[:, first * P : last * P], result[:])
+
+        early = psum.tile([P, 3 * P], F32, name="early")
+        late = psum.tile([P, P], F32, name="late")
+        product(early, 0, 3, "res_early")
+        val_t3 = gather_values(3)
+        quantize_values(3, val_t3)
+        product(late, 3, 4, "res_late")

@@ -27,7 +27,7 @@ def tile_attend_mixedbias_kernel(tc, query, keys_words, keys_scales, bias, gate,
     with ExitStack() as ctx:
         keep = ctx.enter_context(tc.tile_pool(name="keep", bufs=1))
         psum = ctx.enter_context(tc.psum_pool(name="psum", bufs=1))
-        turn = ctx.enter_context(tc.psum_pool(name="turn", bufs=2))
+        turn = ctx.enter_context(tc.psum_pool(name="turn", bufs=3))
 
         slots = keep.tile([P, I // 16], U16, name="slots")
         buckets = keep.tile([P, I // 16], U16, name="buckets")
@@ -37,39 +37,34 @@ def tile_attend_mixedbias_kernel(tc, query, keys_words, keys_scales, bias, gate,
         q_raw = keep.tile([P, PACK, Q], F32, name="q_raw")
         gate_col = keep.tile([P, 1], F32, name="gate_col")
         size_cols = keep.tile([P, PACK], F32, name="size_cols")
-        val_pool = [keep.tile([P, T], F32, name="val_pool%d" % n) for n in range(E_TILES)]
+        val_pool = [keep.tile([P, T], F32, name="val_pool%d" % n, align_bytes=64) for n in range(E_TILES)]
 
         nc.gpsimd.memset(byte_pool[:].bitcast(I32), 0)
-        nc.scalar.dma_start(size_cols[:], size[0].rearrange("(p t) -> p t", t=PACK))
-        nc.scalar.dma_start(gate_col[:], gate)
-        nc.sync.dma_start(buckets[:], offs2)
+        nc.gpsimd.dma_start(gate_col[:], gate)
         nc.sync.dma_start(slots[:], offs)
-        nc.sync.dma_start(bias_pool[:], bias)
+        nc.sync.dma_start(q_raw[:], query.rearrange("(p j) q -> p j q", j=PACK))
         for r in range(4):
             nc.sync.dma_start(byte_pool[r:P:32, :].bitcast(I32), keys_scales[0, r:16:4, :].bitcast(I32))
         nc.sync.dma_start(word_pool[:].bitcast(I32), keys_words[0].rearrange("p n t -> p (n t)").bitcast(I32))
-        nc.sync.dma_start(q_raw[:], query.rearrange("(p j) q -> p j q", j=PACK))
+        nc.sync.dma_start(buckets[:], offs2)
+        nc.sync.dma_start(size_cols[:], size[0].rearrange("(p t) -> p t", t=PACK))
+        nc.sync.dma_start(bias_pool[:], bias)
         for n in range(E_TILES):
             nc.sync.dma_start(val_pool[n][:], vals[n * P : (n + 1) * P, :])
 
         ident = keep.tile([P, P], F32, name="ident")
         make_identity(nc, ident[:])
 
-        bias_g = keep.tile([P, I], F32, name="bias_g")
-        for h in range(2):
-            nc.vector.tensor_copy(
-                bias_g[:, h * 256 : (h + 1) * 256], bias_pool[:].indirect(buckets[:, h * 16 : (h + 1) * 16])
-            )
         k_codes = keep.tile([P, I], U32, name="k_codes", align_bytes=64)
         k_scales = keep.tile([P, I], U8, name="k_scales", align_bytes=64)
         nc.vector.tensor_copy(k_scales[:], byte_pool[:].indirect(slots[:]))
-        nc.vector.tensor_copy(k_codes[:], word_pool[:].indirect(slots[:]))
 
         q_bf = keep.tile([P, Q, PACK], BF16, name="q_bf", align_bytes=64)
         nc.scalar.copy(q_bf[:], q_raw[:].rearrange("p j q -> p q j"))
         q_codes = keep.tile([P, Q], U32, name="q_codes", align_bytes=64)
         q_scales = keep.tile([P, Q], U8, name="q_scales", align_bytes=64)
         nc.vector.quantize_mx(q_codes[:].bitcast(FP8X4), q_scales[:], q_bf[:].rearrange("p q j -> p (q j)"))
+        nc.vector.tensor_copy(k_codes[:], word_pool[:].indirect(slots[:]))
 
         scores = psum.tile([P, I], F32, name="scores")
         nc.tensor.matmul_mx(
@@ -82,101 +77,100 @@ def tile_attend_mixedbias_kernel(tc, query, keys_words, keys_scales, bias, gate,
             stop=True,
         )
 
+        bias_g = keep.tile([P, I], F32, name="bias_g")
+        for h in range(2):
+            nc.vector.tensor_copy(
+                bias_g[:, h * 256 : (h + 1) * 256], bias_pool[:].indirect(buckets[:, h * 16 : (h + 1) * 16])
+            )
+
         size_rows = psum.tile([P, PACK, P], F32, name="size_rows")
         for t in range(PACK):
             nc.tensor.transpose(size_rows[:, t, :], size_cols[:, t : t + 1].to_broadcast([P, P]), ident[:])
-        rest_col = keep.tile([P, 1], F32, name="rest_col")
-        nc.vector.tensor_scalar(rest_col[:], gate_col[:], -1.0, 1.0, ALU.mult, ALU.add)
 
-        v_codes = keep.tile([P, E], U32, name="v_codes", align_bytes=64)
-        v_scales = keep.tile([P, E], U8, name="v_scales", align_bytes=64)
-
-        def turn_pairs(rows_bf, name):
+        def turn_pairs(rows_bf, grouped):
             words = rows_bf[:].bitcast(F32)
             turned = turn.tile([P, 2, P], F32, name="turned")
             for u in range(2):
                 nc.tensor.transpose(turned[:, u, :], words[:, u : I // 2 : 2], ident[:])
-            grouped = keep.tile([P, P * PACK], BF16, name=name, align_bytes=64)
             nc.scalar.copy(
-                grouped[:].bitcast(F32).rearrange("p (x u) -> p x u", u=2), turned[:].rearrange("p u x -> p x u")
+                grouped.bitcast(F32).rearrange("p (x u) -> p x u", u=2), turned[:].rearrange("p u x -> p x u")
             )
-            return grouped
 
-        def gather_values(n):
-            val_g = keep.tile([P, I], BF16, name="val_g%d" % n)
+        def gather_values(n, grouped, slot):
+            val_g = keep.tile([P, I], BF16, name="val_g%d" % n, tag=slot)
             nc.vector.tensor_copy(val_g[:], val_pool[n][:].indirect(slots[:]))
-            return turn_pairs(val_g, "val_t%d" % n)
+            turn_pairs(val_g, grouped)
 
-        def quantize_values(n, grouped):
-            cols = slice(n * P, (n + 1) * P)
-            nc.vector.quantize_mx(v_codes[:, cols].bitcast(FP8X4), v_scales[:, cols], grouped[:])
+        early_bf = keep.tile([P, E_TILES * I], BF16, name="early_bf", align_bytes=64)
+        late_bf = keep.tile([P, I], BF16, name="late_bf", align_bytes=64)
 
         biased = keep.tile([P, I], F32, name="biased")
-        nc.vector.tensor_tensor(biased[:], scores[:], bias_g[:], ALU.add)
+        for h in range(2):
+            half = slice(h * 256, (h + 1) * 256)
+            nc.vector.tensor_tensor(biased[:, half], scores[:, half], bias_g[:, half], ALU.add)
         neg_max_r = keep.tile([P, 1], F32, name="neg_max_r")
         neg_max_p = keep.tile([P, 1], F32, name="neg_max_p")
-        nc.vector.tensor_reduce(neg_max_r[:], scores[:], AXIS_X, ALU.max, negate=True)
-        nc.vector.tensor_reduce(neg_max_p[:], biased[:], AXIS_X, ALU.max, negate=True)
         exp_r = keep.tile([P, I], F32, name="exp_r")
         exp_p = keep.tile([P, I], F32, name="exp_p")
-        sum_r = keep.tile([P, 1], F32, name="sum_r")
-        sum_p = keep.tile([P, 1], F32, name="sum_p")
-        nc.scalar.activation(exp_r[:], scores[:], ACT.Exp, bias=neg_max_r[:], accum_out=sum_r[:])
-        nc.scalar.activation(exp_p[:], biased[:], ACT.Exp, bias=neg_max_p[:], accum_out=sum_p[:])
+        sums = keep.tile([P, 2], F32, name="sums")
+        nc.vector.tensor_reduce(neg_max_r[:], scores[:], AXIS_X, ALU.max, negate=True)
+        nc.vector.tensor_reduce(neg_max_p[:], biased[:], AXIS_X, ALU.max, negate=True)
+        nc.scalar.activation(exp_r[:], scores[:], ACT.Exp, bias=neg_max_r[:], accum_out=sums[:, 1:2])
+        nc.scalar.activation(exp_p[:], biased[:], ACT.Exp, bias=neg_max_p[:], accum_out=sums[:, 0:1])
 
-        val_t0 = gather_values(0)
+        gather_values(0, early_bf[:, I : 2 * I], "val_g0")
 
-        inv_r = keep.tile([P, 1], F32, name="inv_r")
-        inv_p = keep.tile([P, 1], F32, name="inv_p")
-        mix_r = keep.tile([P, 1], F32, name="mix_r")
-        mix_p = keep.tile([P, 1], F32, name="mix_p")
-        nc.vector.reciprocal(inv_r[:], sum_r[:])
-        nc.vector.reciprocal(inv_p[:], sum_p[:])
-        nc.vector.tensor_tensor(mix_r[:], inv_r[:], rest_col[:], ALU.mult)
-        nc.vector.tensor_tensor(mix_p[:], inv_p[:], gate_col[:], ALU.mult)
+        inverse = keep.tile([P, 2], F32, name="inverse", align_bytes=64)
+        mix = keep.tile([P, 2], F32, name="mix")
+        nc.vector.reciprocal(inverse[:], sums[:])
+        rest_col = keep.tile([P, 1], F32, name="rest_col")
+        nc.scalar.activation(rest_col[:], gate_col[:], ACT.Copy, scale=-1.0, bias=1.0)
+        nc.scalar.activation(mix[:, 1:2], inverse[:, 1:2], ACT.Copy, scale=rest_col[:])
+        nc.scalar.activation(mix[:, 0:1], inverse[:, 0:1], ACT.Copy, scale=gate_col[:])
         part_r = keep.tile([P, I], F32, name="part_r")
-        nc.scalar.activation(part_r[:], exp_r[:], ACT.Copy, scale=mix_r[:])
+        nc.scalar.activation(part_r[:], exp_r[:], ACT.Copy, scale=mix[:, 1:2])
 
-        val_t1 = gather_values(1)
-        quantize_values(0, val_t0)
+        gather_values(1, early_bf[:, 2 * I : 3 * I], "biased")
 
-        mixed = keep.tile([P, I], F32, name="mixed")
-        nc.vector.scalar_tensor_tensor(mixed[:], exp_p[:], mix_p[:], part_r[:], ALU.mult, ALU.add)
-        w_bf = keep.tile([P, I], BF16, name="w_bf")
+        mixed = keep.tile([P, I], F32, name="mixed", tag="val_pool1", align_bytes=64)
+        nc.vector.scalar_tensor_tensor(mixed[:], exp_p[:], mix[:, 0:1], part_r[:], ALU.mult, ALU.add)
+        gather_values(2, early_bf[:, 3 * I : 4 * I], "exp_r")
+        w_bf = keep.tile([P, I], BF16, name="w_bf", tag="val_pool2", align_bytes=64)
         nc.vector.tensor_tensor(
             w_bf[:].rearrange("p (n t) -> p n t", t=PACK),
             size_rows[:].rearrange("p t n -> p n t"),
             mixed[:].rearrange("p (n t) -> p n t", t=PACK),
             ALU.mult,
         )
-        w_t = turn_pairs(w_bf, "w_t")
-        quantize_values(1, val_t1)
-        val_t2 = gather_values(2)
-        w_codes = keep.tile([P, Q], U32, name="w_codes", align_bytes=64)
-        w_scales = keep.tile([P, Q], U8, name="w_scales", align_bytes=64)
-        nc.vector.quantize_mx(w_codes[:].bitcast(FP8X4), w_scales[:], w_t[:])
-        quantize_values(2, val_t2)
+        turn_pairs(w_bf, early_bf[:, 0:I])
+        gather_values(3, late_bf[:], "part_r")
 
-        def product(acc, first, last, name):
-            base = first * P
-            for lo, hi in ((c, min(c + 2, last)) for c in range(first, last, 2)):
-                cols = slice(lo * P, hi * P)
-                nc.tensor.matmul_mx(
-                    acc[:, lo * P - base : hi * P - base],
-                    lhsT=w_codes[:].bitcast(FP8X4),
-                    lhsT_scale=w_scales[:],
-                    rhs=v_codes[:, cols].bitcast(FP8X4),
-                    rhs_scale=v_scales[:, cols],
-                    start=True,
-                    stop=True,
-                )
-            result = keep.tile([P, (last - first) * P], F32, name=name)
-            nc.scalar.copy(result[:], acc[:])
-            nc.sync.dma_start(out[:, first * P : last * P], result[:])
+        early_codes = keep.tile([P, E_TILES * P], U32, name="early_codes", tag="val_pool3", align_bytes=64)
+        early_scales = keep.tile([P, E_TILES * P], U8, name="early_scales", align_bytes=64)
+        nc.vector.quantize_mx(early_codes[:].bitcast(FP8X4), early_scales[:], early_bf[:])
+        late_codes = keep.tile([P, P], U32, name="late_codes", align_bytes=64)
+        late_scales = keep.tile([P, P], U8, name="late_scales", align_bytes=64)
+        nc.vector.quantize_mx(late_codes[:].bitcast(FP8X4), late_scales[:], late_bf[:])
 
-        early = psum.tile([P, 3 * P], F32, name="early")
-        late = psum.tile([P, P], F32, name="late")
-        product(early, 0, 3, "res_early")
-        val_t3 = gather_values(3)
-        quantize_values(3, val_t3)
-        product(late, 3, 4, "res_late")
+        def product(acc, codes, scales):
+            nc.tensor.matmul_mx(
+                acc,
+                lhsT=early_codes[:, 0:Q].bitcast(FP8X4),
+                lhsT_scale=early_scales[:, 0:Q],
+                rhs=codes.bitcast(FP8X4),
+                rhs_scale=scales,
+                start=True,
+                stop=True,
+            )
+
+        early_acc = psum.tile([P, 3 * P], F32, name="early_acc")
+        late_acc = psum.tile([P, P], F32, name="late_acc")
+        product(early_acc[:, 0 : 2 * P], early_codes[:, P : 3 * P], early_scales[:, P : 3 * P])
+        product(early_acc[:, 2 * P : 3 * P], early_codes[:, 3 * P : 4 * P], early_scales[:, 3 * P : 4 * P])
+        product(late_acc[:], late_codes[:], late_scales[:])
+        early_out = keep.tile([P, 3 * P], F32, name="early_out")
+        late_out = keep.tile([P, P], F32, name="late_out")
+        nc.scalar.copy(early_out[:], early_acc[:])
+        nc.sync.dma_start(out[:, 0 : 3 * P], early_out[:])
+        nc.vector.tensor_copy(late_out[:], late_acc[:])
+        nc.sync.dma_start(out[:, 3 * P : 4 * P], late_out[:])

@@ -83,10 +83,6 @@ def tile_attend_mixedbias_kernel(tc, query, keys_words, keys_scales, bias, gate,
                 bias_g[:, h * 256 : (h + 1) * 256], bias_pool[:].indirect(buckets[:, h * 16 : (h + 1) * 16])
             )
 
-        size_rows = psum.tile([P, PACK, P], F32, name="size_rows")
-        for t in range(PACK):
-            nc.tensor.transpose(size_rows[:, t, :], size_cols[:, t : t + 1].to_broadcast([P, P]), ident[:])
-
         def turn_pairs(rows_bf, grouped):
             words = rows_bf[:].bitcast(F32)
             turned = turn.tile([P, 2, P], F32, name="turned")
@@ -101,24 +97,30 @@ def tile_attend_mixedbias_kernel(tc, query, keys_words, keys_scales, bias, gate,
             nc.vector.tensor_copy(val_g[:], val_pool[n][:].indirect(slots[:]))
             turn_pairs(val_g, grouped)
 
-        early_bf = keep.tile([P, E_TILES * I], BF16, name="early_bf", align_bytes=64)
+        early_bf = keep.tile([P, E_TILES * I], BF16, name="early_bf", tag="val_pool2", align_bytes=64)
         late_bf = keep.tile([P, I], BF16, name="late_bf", align_bytes=64)
 
         biased = keep.tile([P, I], F32, name="biased")
-        for h in range(2):
-            half = slice(h * 256, (h + 1) * 256)
-            nc.vector.tensor_tensor(biased[:, half], scores[:, half], bias_g[:, half], ALU.add)
+        nc.vector.tensor_tensor(biased[:], scores[:], bias_g[:], ALU.add)
         neg_max_r = keep.tile([P, 1], F32, name="neg_max_r")
         neg_max_p = keep.tile([P, 1], F32, name="neg_max_p")
-        exp_r = keep.tile([P, I], F32, name="exp_r")
-        exp_p = keep.tile([P, I], F32, name="exp_p")
+        exp_r = keep.tile([P, PACK, P], F32, name="exp_r")
+        exp_p = keep.tile([P, PACK, P], F32, name="exp_p")
         sums = keep.tile([P, 2], F32, name="sums")
         nc.vector.tensor_reduce(neg_max_r[:], scores[:], AXIS_X, ALU.max, negate=True)
         nc.vector.tensor_reduce(neg_max_p[:], biased[:], AXIS_X, ALU.max, negate=True)
-        nc.scalar.activation(exp_r[:], scores[:], ACT.Exp, bias=neg_max_r[:], accum_out=sums[:, 1:2])
-        nc.scalar.activation(exp_p[:], biased[:], ACT.Exp, bias=neg_max_p[:], accum_out=sums[:, 0:1])
+        nc.scalar.activation(
+            exp_r[:], scores[:].rearrange("p (s t) -> p t s", t=PACK), ACT.Exp, bias=neg_max_r[:], accum_out=sums[:, 1:2]
+        )
+        nc.scalar.activation(
+            exp_p[:].rearrange("p t (c j) -> p c t j", j=4),
+            biased[:].rearrange("p (c j t) -> p c t j", j=4, t=PACK),
+            ACT.Exp,
+            bias=neg_max_p[:],
+            accum_out=sums[:, 0:1],
+        )
 
-        gather_values(0, early_bf[:, I : 2 * I], "val_g0")
+        gather_values(0, early_bf[:, I : 2 * I], "bias_g")
 
         inverse = keep.tile([P, 2], F32, name="inverse", align_bytes=64)
         mix = keep.tile([P, 2], F32, name="mix")
@@ -127,23 +129,31 @@ def tile_attend_mixedbias_kernel(tc, query, keys_words, keys_scales, bias, gate,
         nc.scalar.activation(rest_col[:], gate_col[:], ACT.Copy, scale=-1.0, bias=1.0)
         nc.scalar.activation(mix[:, 1:2], inverse[:, 1:2], ACT.Copy, scale=rest_col[:])
         nc.scalar.activation(mix[:, 0:1], inverse[:, 0:1], ACT.Copy, scale=gate_col[:])
-        part_r = keep.tile([P, I], F32, name="part_r")
+        part_r = keep.tile([P, PACK, P], F32, name="part_r")
+        part_p = keep.tile([P, PACK, P], F32, name="part_p")
         nc.scalar.activation(part_r[:], exp_r[:], ACT.Copy, scale=mix[:, 1:2])
+        nc.scalar.activation(part_p[:], exp_p[:], ACT.Copy, scale=mix[:, 0:1])
+        mixed = psum.tile([P, PACK, P], F32, name="mixed")
+        for k, part in enumerate((part_r, part_p)):
+            for t in range(PACK):
+                nc.tensor.matmul(
+                    mixed[:, t, :],
+                    part[:, t, :],
+                    ident[:],
+                    start=(k == 0 and t == 0),
+                    stop=(k == 1 and t == PACK - 1),
+                    is_transpose=True,
+                )
 
-        gather_values(1, early_bf[:, 2 * I : 3 * I], "biased")
-
-        mixed = keep.tile([P, I], F32, name="mixed", tag="val_pool1", align_bytes=64)
-        nc.vector.scalar_tensor_tensor(mixed[:], exp_p[:], mix[:, 0:1], part_r[:], ALU.mult, ALU.add)
-        gather_values(2, early_bf[:, 3 * I : 4 * I], "exp_r")
-        w_bf = keep.tile([P, I], BF16, name="w_bf", tag="val_pool2", align_bytes=64)
+        gather_values(1, early_bf[:, 2 * I : 3 * I], "val_g1")
         nc.vector.tensor_tensor(
-            w_bf[:].rearrange("p (n t) -> p n t", t=PACK),
-            size_rows[:].rearrange("p t n -> p n t"),
-            mixed[:].rearrange("p (n t) -> p n t", t=PACK),
+            early_bf[:, 0:I].rearrange("p (q t) -> p q t", t=PACK),
+            mixed[:].rearrange("p t q -> p q t"),
+            size_cols[:].unsqueeze(1).to_broadcast([P, Q, PACK]),
             ALU.mult,
         )
-        turn_pairs(w_bf, early_bf[:, 0:I])
-        gather_values(3, late_bf[:], "part_r")
+        gather_values(2, early_bf[:, 3 * I : 4 * I], "val_g2")
+        gather_values(3, late_bf[:], "val_g3")
 
         early_codes = keep.tile([P, E_TILES * P], U32, name="early_codes", tag="val_pool3", align_bytes=64)
         early_scales = keep.tile([P, E_TILES * P], U8, name="early_scales", align_bytes=64)

@@ -46,11 +46,12 @@ def tile_attend_mixedbias_kernel(tc, query, keys_words, keys_scales, bias, gate,
         for r in range(4):
             nc.sync.dma_start(byte_pool[r:P:32, :].bitcast(I32), keys_scales[0, r:16:4, :].bitcast(I32))
         nc.sync.dma_start(word_pool[:].bitcast(I32), keys_words[0].rearrange("p n t -> p (n t)").bitcast(I32))
-        nc.sync.dma_start(buckets[:], offs2)
-        nc.sync.dma_start(size_cols[:], size[0].rearrange("(p t) -> p t", t=PACK))
         nc.sync.dma_start(bias_pool[:], bias)
+        nc.sync.dma_start(buckets[:], offs2)
         for n in range(E_TILES):
             nc.sync.dma_start(val_pool[n][:], vals[n * P : (n + 1) * P, :])
+            if n == 0:
+                nc.sync.dma_start(size_cols[:], size[0].rearrange("(p t) -> p t", t=PACK))
 
         ident = keep.tile([P, P], F32, name="ident")
         make_identity(nc, ident[:])

@@ -20,6 +20,7 @@ AXIS_X = mybir.AxisListType.X
 P = 128
 PACK = 4
 E_TILES = E // P
+HALF = I // 2
 
 
 def tile_attend_mixedbias_kernel(tc, query, keys_words, keys_scales, bias, gate, size, vals, offs, offs2, out):
@@ -41,13 +42,13 @@ def tile_attend_mixedbias_kernel(tc, query, keys_words, keys_scales, bias, gate,
 
         nc.gpsimd.memset(byte_pool[:].bitcast(I32), 0)
         nc.gpsimd.dma_start(gate_col[:], gate)
+        nc.sync.dma_start(buckets[:], offs2)
+        nc.sync.dma_start(bias_pool[:], bias)
         nc.sync.dma_start(slots[:], offs)
         nc.sync.dma_start(q_raw[:], query.rearrange("(p j) q -> p j q", j=PACK))
         for r in range(4):
             nc.sync.dma_start(byte_pool[r:P:32, :].bitcast(I32), keys_scales[0, r:16:4, :].bitcast(I32))
         nc.sync.dma_start(word_pool[:].bitcast(I32), keys_words[0].rearrange("p n t -> p (n t)").bitcast(I32))
-        nc.sync.dma_start(bias_pool[:], bias)
-        nc.sync.dma_start(buckets[:], offs2)
         for n in range(E_TILES):
             nc.sync.dma_start(val_pool[n][:], vals[n * P : (n + 1) * P, :])
             if n == 0:
@@ -55,6 +56,12 @@ def tile_attend_mixedbias_kernel(tc, query, keys_words, keys_scales, bias, gate,
 
         ident = keep.tile([P, P], F32, name="ident")
         make_identity(nc, ident[:])
+
+        bias_g = keep.tile([P, I], F32, name="bias_g")
+        for h in range(2):
+            nc.vector.tensor_copy(
+                bias_g[:, h * 256 : (h + 1) * 256], bias_pool[:].indirect(buckets[:, h * 16 : (h + 1) * 16])
+            )
 
         k_codes = keep.tile([P, I], U32, name="k_codes", align_bytes=64)
         k_scales = keep.tile([P, I], U8, name="k_scales", align_bytes=64)
@@ -65,23 +72,19 @@ def tile_attend_mixedbias_kernel(tc, query, keys_words, keys_scales, bias, gate,
         q_codes = keep.tile([P, Q], U32, name="q_codes", align_bytes=64)
         q_scales = keep.tile([P, Q], U8, name="q_scales", align_bytes=64)
         nc.vector.quantize_mx(q_codes[:].bitcast(FP8X4), q_scales[:], q_bf[:].rearrange("p q j -> p (q j)"))
-        nc.vector.tensor_copy(k_codes[:], word_pool[:].indirect(slots[:]))
-
-        scores = psum.tile([P, I], F32, name="scores")
-        nc.tensor.matmul_mx(
-            scores[:],
-            lhsT=q_codes[:].bitcast(FP8X4),
-            lhsT_scale=q_scales[:],
-            rhs=k_codes[:].bitcast(FP8X4),
-            rhs_scale=k_scales[:],
-            start=True,
-            stop=True,
-        )
-
-        bias_g = keep.tile([P, I], F32, name="bias_g")
+        halves = [slice(h * HALF, (h + 1) * HALF) for h in range(2)]
+        scores = []
         for h in range(2):
-            nc.vector.tensor_copy(
-                bias_g[:, h * 256 : (h + 1) * 256], bias_pool[:].indirect(buckets[:, h * 16 : (h + 1) * 16])
+            nc.vector.tensor_copy(k_codes[:, halves[h]], word_pool[:].indirect(slots[:, h * 16 : (h + 1) * 16]))
+            scores.append(psum.tile([P, HALF], F32, name="scores%d" % h))
+            nc.tensor.matmul_mx(
+                scores[h][:],
+                lhsT=q_codes[:].bitcast(FP8X4),
+                lhsT_scale=q_scales[:],
+                rhs=k_codes[:, halves[h]].bitcast(FP8X4),
+                rhs_scale=k_scales[:, halves[h]],
+                start=True,
+                stop=True,
             )
 
         def turn_pairs(rows_bf, grouped):
@@ -102,40 +105,44 @@ def tile_attend_mixedbias_kernel(tc, query, keys_words, keys_scales, bias, gate,
         late_bf = keep.tile([P, I], BF16, name="late_bf", align_bytes=64)
 
         biased = keep.tile([P, I], F32, name="biased")
-        nc.vector.tensor_tensor(biased[:], scores[:], bias_g[:], ALU.add)
+        negated = keep.tile([P, I], F32, name="negated")
+        first_min = keep.tile([P, 1], F32, name="first_min")
         neg_max_r = keep.tile([P, 1], F32, name="neg_max_r")
         neg_max_p = keep.tile([P, 1], F32, name="neg_max_p")
         exp_r = keep.tile([P, PACK, P], F32, name="exp_r")
         exp_p = keep.tile([P, PACK, P], F32, name="exp_p")
         sums = keep.tile([P, 2], F32, name="sums")
-        nc.vector.tensor_reduce(neg_max_r[:], scores[:], AXIS_X, ALU.max, negate=True)
+        nc.vector.tensor_scalar(negated[:, halves[0]], scores[0][:], -1.0, None, ALU.mult, ALU.min, accum_out=first_min[:])
+        for h in range(2):
+            nc.vector.tensor_tensor(biased[:, halves[h]], scores[h][:], bias_g[:, halves[h]], ALU.add)
+        nc.vector.tensor_scalar(
+            negated[:, halves[1]], scores[1][:], -1.0, first_min[:], ALU.mult, ALU.min, accum_out=neg_max_r[:]
+        )
         nc.vector.tensor_reduce(neg_max_p[:], biased[:], AXIS_X, ALU.max, negate=True)
-        nc.scalar.activation(
-            exp_r[:], scores[:].rearrange("p (s t) -> p t s", t=PACK), ACT.Exp, bias=neg_max_r[:], accum_out=sums[:, 1:2]
-        )
-        nc.scalar.activation(
-            exp_p[:].rearrange("p t (c j) -> p c t j", j=4),
-            biased[:].rearrange("p (c j t) -> p c t j", j=4, t=PACK),
-            ACT.Exp,
-            bias=neg_max_p[:],
-            accum_out=sums[:, 0:1],
-        )
+        for exps, source, sign, neg_max, column in ((exp_r, negated, -1.0, neg_max_r, 1), (exp_p, biased, 1.0, neg_max_p, 0)):
+            nc.scalar.activation(
+                exps[:].rearrange("p t (c j) -> p c t j", j=4),
+                source[:].rearrange("p (c j t) -> p c t j", j=4, t=PACK),
+                ACT.Exp,
+                bias=neg_max[:],
+                scale=sign,
+                accum_out=sums[:, column : column + 1],
+            )
 
         gather_values(0, early_bf[:, I : 2 * I], "bias_g")
 
         inverse = keep.tile([P, 2], F32, name="inverse", align_bytes=64)
-        mix = keep.tile([P, 2], F32, name="mix")
+        mix = keep.tile([P, 1], F32, name="mix")
         nc.vector.reciprocal(inverse[:], sums[:])
-        rest_col = keep.tile([P, 1], F32, name="rest_col")
+        rest_col = keep.tile([P, 1], F32, name="rest_col", tag="q_raw")
         nc.scalar.activation(rest_col[:], gate_col[:], ACT.Copy, scale=-1.0, bias=1.0)
-        nc.scalar.activation(mix[:, 1:2], inverse[:, 1:2], ACT.Copy, scale=rest_col[:])
-        nc.scalar.activation(mix[:, 0:1], inverse[:, 0:1], ACT.Copy, scale=gate_col[:])
+        nc.scalar.activation(mix[:], inverse[:, 1:2], ACT.Copy, scale=rest_col[:])
         part_r = keep.tile([P, PACK, P], F32, name="part_r")
         part_p = keep.tile([P, PACK, P], F32, name="part_p")
-        nc.scalar.activation(part_r[:], exp_r[:], ACT.Copy, scale=mix[:, 1:2])
-        nc.scalar.activation(part_p[:], exp_p[:], ACT.Copy, scale=mix[:, 0:1])
+        nc.scalar.activation(part_r[:], exp_r[:], ACT.Copy, scale=mix[:])
+        nc.vector.tensor_scalar(part_p[:], exp_p[:], inverse[:, 0:1], gate_col[:], ALU.mult, ALU.mult)
         mixed = psum.tile([P, PACK, P], F32, name="mixed")
-        for k, part in enumerate((part_r, part_p)):
+        for k, part in enumerate((part_p, part_r)):
             for t in range(PACK):
                 nc.tensor.matmul(
                     mixed[:, t, :],

@@ -21,6 +21,7 @@ P = 128
 PACK = 4
 E_TILES = E // P
 HALF = I // 2
+RUN = 16
 
 
 def tile_attend_mixedbias_kernel(tc, query, keys_words, keys_scales, bias, gate, size, vals, offs, offs2, out):
@@ -37,10 +38,12 @@ def tile_attend_mixedbias_kernel(tc, query, keys_words, keys_scales, bias, gate,
         byte_pool = keep.tile([P, T], U8, name="byte_pool")
         q_raw = keep.tile([P, PACK, Q], F32, name="q_raw")
         gate_col = keep.tile([P, 1], F32, name="gate_col")
-        size_cols = keep.tile([P, PACK], F32, name="size_cols")
+        size_rows = keep.tile([P, HALF], F32, name="size_rows")
+        size_cols = keep.tile([P, 2, 2], F32, name="size_cols")
         val_pool = [keep.tile([P, T], F32, name="val_pool%d" % n, align_bytes=64) for n in range(E_TILES)]
 
         nc.gpsimd.memset(byte_pool[:].bitcast(I32), 0)
+        nc.gpsimd.memset(size_rows[:], 0.0)
         nc.gpsimd.dma_start(gate_col[:], gate)
         nc.sync.dma_start(buckets[:], offs2)
         nc.sync.dma_start(bias_pool[:], bias)
@@ -52,7 +55,9 @@ def tile_attend_mixedbias_kernel(tc, query, keys_words, keys_scales, bias, gate,
         for n in range(E_TILES):
             nc.sync.dma_start(val_pool[n][:], vals[n * P : (n + 1) * P, :])
             if n == 0:
-                nc.sync.dma_start(size_cols[:], size[0].rearrange("(p t) -> p t", t=PACK))
+                nc.sync.dma_start(
+                    size_rows[0:2, :].rearrange("h (g r) -> h g r", r=RUN), size[0].rearrange("(g h r) -> h g r", h=2, r=RUN)
+                )
 
         ident = keep.tile([P, P], F32, name="ident")
         make_identity(nc, ident[:])
@@ -87,18 +92,26 @@ def tile_attend_mixedbias_kernel(tc, query, keys_words, keys_scales, bias, gate,
                 stop=True,
             )
 
+        def dealt(tile):
+            return tile[:].rearrange("p (h g r) -> p g h r", h=2, r=RUN)
+
+        size_turned = psum.tile([P, 2, P], F32, name="size_turned", tag="mixed")
+        for e in range(2):
+            nc.tensor.transpose(size_turned[:, e, :], size_rows[:, e:HALF:2], ident[:])
+        nc.scalar.copy(size_cols[:], size_turned[:, :, 0:2].rearrange("p e h -> p h e"))
+
         def turn_pairs(rows_bf, grouped):
             words = rows_bf[:].bitcast(F32)
             turned = turn.tile([P, 2, P], F32, name="turned")
             for u in range(2):
-                nc.tensor.transpose(turned[:, u, :], words[:, u : I // 2 : 2], ident[:])
+                nc.tensor.transpose(turned[:, u, :], words[:, u * P : (u + 1) * P], ident[:])
             nc.scalar.copy(
                 grouped.bitcast(F32).rearrange("p (x u) -> p x u", u=2), turned[:].rearrange("p u x -> p x u")
             )
 
         def gather_values(n, grouped, slot):
             val_g = keep.tile([P, I], BF16, name="val_g%d" % n, tag=slot)
-            nc.vector.tensor_copy(val_g[:], val_pool[n][:].indirect(slots[:]))
+            nc.vector.tensor_copy(dealt(val_g), val_pool[n][:].indirect(slots[:]))
             turn_pairs(val_g, grouped)
 
         early_bf = keep.tile([P, E_TILES * I], BF16, name="early_bf", tag="val_pool2", align_bytes=64)
@@ -109,8 +122,8 @@ def tile_attend_mixedbias_kernel(tc, query, keys_words, keys_scales, bias, gate,
         first_min = keep.tile([P, 1], F32, name="first_min")
         neg_max_r = keep.tile([P, 1], F32, name="neg_max_r")
         neg_max_p = keep.tile([P, 1], F32, name="neg_max_p")
-        exp_r = keep.tile([P, PACK, P], F32, name="exp_r")
-        exp_p = keep.tile([P, PACK, P], F32, name="exp_p")
+        exp_r = keep.tile([P, I], F32, name="exp_r")
+        exp_p = keep.tile([P, I], F32, name="exp_p")
         sums = keep.tile([P, 2], F32, name="sums")
         nc.vector.tensor_scalar(negated[:, halves[0]], scores[0][:], -1.0, None, ALU.mult, ALU.min, accum_out=first_min[:])
         for h in range(2):
@@ -121,8 +134,8 @@ def tile_attend_mixedbias_kernel(tc, query, keys_words, keys_scales, bias, gate,
         nc.vector.tensor_reduce(neg_max_p[:], biased[:], AXIS_X, ALU.max, negate=True)
         for exps, source, sign, neg_max, column in ((exp_r, negated, -1.0, neg_max_r, 1), (exp_p, biased, 1.0, neg_max_p, 0)):
             nc.scalar.activation(
-                exps[:].rearrange("p t (c j) -> p c t j", j=4),
-                source[:].rearrange("p (c j t) -> p c t j", j=4, t=PACK),
+                dealt(exps),
+                source[:].rearrange("p (g h r) -> p g h r", h=2, r=RUN),
                 ACT.Exp,
                 bias=neg_max[:],
                 scale=sign,
@@ -137,8 +150,8 @@ def tile_attend_mixedbias_kernel(tc, query, keys_words, keys_scales, bias, gate,
         rest_col = keep.tile([P, 1], F32, name="rest_col", tag="q_raw")
         nc.scalar.activation(rest_col[:], gate_col[:], ACT.Copy, scale=-1.0, bias=1.0)
         nc.scalar.activation(mix[:], inverse[:, 1:2], ACT.Copy, scale=rest_col[:])
-        part_r = keep.tile([P, PACK, P], F32, name="part_r")
-        part_p = keep.tile([P, PACK, P], F32, name="part_p")
+        part_r = keep.tile([P, I], F32, name="part_r")
+        part_p = keep.tile([P, I], F32, name="part_p")
         nc.scalar.activation(part_r[:], exp_r[:], ACT.Copy, scale=mix[:])
         nc.vector.tensor_scalar(part_p[:], exp_p[:], inverse[:, 0:1], gate_col[:], ALU.mult, ALU.mult)
         mixed = psum.tile([P, PACK, P], F32, name="mixed")
@@ -146,7 +159,7 @@ def tile_attend_mixedbias_kernel(tc, query, keys_words, keys_scales, bias, gate,
             for t in range(PACK):
                 nc.tensor.matmul(
                     mixed[:, t, :],
-                    part[:, t, :],
+                    part[:, (t // 2) * HALF + t % 2 : (t // 2 + 1) * HALF : 2],
                     ident[:],
                     start=(k == 0 and t == 0),
                     stop=(k == 1 and t == PACK - 1),
@@ -157,7 +170,7 @@ def tile_attend_mixedbias_kernel(tc, query, keys_words, keys_scales, bias, gate,
         nc.vector.tensor_tensor(
             early_bf[:, 0:I].rearrange("p (q t) -> p q t", t=PACK),
             mixed[:].rearrange("p t q -> p q t"),
-            size_cols[:].unsqueeze(1).to_broadcast([P, Q, PACK]),
+            size_cols[:].rearrange("p h e -> p (h e)").unsqueeze(1).to_broadcast([P, Q, PACK]),
             ALU.mult,
         )
         gather_values(2, early_bf[:, 3 * I : 4 * I], "val_g2")
@@ -165,14 +178,20 @@ def tile_attend_mixedbias_kernel(tc, query, keys_words, keys_scales, bias, gate,
 
         early_codes = keep.tile([P, E_TILES * P], U32, name="early_codes", tag="val_pool3", align_bytes=64)
         early_scales = keep.tile([P, E_TILES * P], U8, name="early_scales", align_bytes=64)
-        nc.vector.quantize_mx(early_codes[:].bitcast(FP8X4), early_scales[:], early_bf[:])
+        for h in range(2):
+            cols = slice(h * 2 * P, (h + 1) * 2 * P)
+            nc.vector.quantize_mx(
+                early_codes[:, cols].bitcast(FP8X4), early_scales[:, cols], early_bf[:, h * 2 * I : (h + 1) * 2 * I]
+            )
         late_codes = keep.tile([P, P], U32, name="late_codes", align_bytes=64)
         late_scales = keep.tile([P, P], U8, name="late_scales", align_bytes=64)
         nc.vector.quantize_mx(late_codes[:].bitcast(FP8X4), late_scales[:], late_bf[:])
 
-        def product(acc, codes, scales):
+        def finish(name, codes, scales, first, copy, bank):
+            width = codes.shape[1]
+            acc = psum.tile([P, width], F32, name=name + "_acc", tag=bank)
             nc.tensor.matmul_mx(
-                acc,
+                acc[:],
                 lhsT=early_codes[:, 0:Q].bitcast(FP8X4),
                 lhsT_scale=early_scales[:, 0:Q],
                 rhs=codes.bitcast(FP8X4),
@@ -180,15 +199,10 @@ def tile_attend_mixedbias_kernel(tc, query, keys_words, keys_scales, bias, gate,
                 start=True,
                 stop=True,
             )
+            result = keep.tile([P, width], F32, name=name + "_out")
+            copy(result[:], acc[:])
+            nc.sync.dma_start(out[:, first : first + width], result[:])
 
-        early_acc = psum.tile([P, 3 * P], F32, name="early_acc")
-        late_acc = psum.tile([P, P], F32, name="late_acc")
-        product(early_acc[:, 0 : 2 * P], early_codes[:, P : 3 * P], early_scales[:, P : 3 * P])
-        product(early_acc[:, 2 * P : 3 * P], early_codes[:, 3 * P : 4 * P], early_scales[:, 3 * P : 4 * P])
-        product(late_acc[:], late_codes[:], late_scales[:])
-        early_out = keep.tile([P, 3 * P], F32, name="early_out")
-        late_out = keep.tile([P, P], F32, name="late_out")
-        nc.scalar.copy(early_out[:], early_acc[:])
-        nc.sync.dma_start(out[:, 0 : 3 * P], early_out[:])
-        nc.vector.tensor_copy(late_out[:], late_acc[:])
-        nc.sync.dma_start(out[:, 3 * P : 4 * P], late_out[:])
+        finish("early", early_codes[:, P : 2 * P], early_scales[:, P : 2 * P], 0, nc.scalar.copy, "scores0")
+        finish("mid", early_codes[:, 2 * P : 4 * P], early_scales[:, 2 * P : 4 * P], P, nc.scalar.copy, "mid_acc")
+        finish("late", late_codes[:], late_scales[:], 3 * P, nc.vector.tensor_copy, "late_acc")

@@ -22,6 +22,9 @@ PACK = 4
 E_TILES = E // P
 HALF = I // 2
 RUN = 16
+LIST_COLS = I // 16
+LAST_PIECES = 2
+PIECE = P // LAST_PIECES
 
 
 def tile_attend_mixedbias_kernel(tc, query, keys_words, keys_scales, bias, gate, size, vals, offs, offs2, out):
@@ -31,8 +34,8 @@ def tile_attend_mixedbias_kernel(tc, query, keys_words, keys_scales, bias, gate,
         psum = ctx.enter_context(tc.psum_pool(name="psum", bufs=1))
         turn = ctx.enter_context(tc.psum_pool(name="turn", bufs=3))
 
-        slots = keep.tile([P, I // 16], U16, name="slots")
-        buckets = keep.tile([P, I // 16], U16, name="buckets")
+        slots = keep.tile([P, LIST_COLS], U16, name="slots")
+        buckets = keep.tile([P, LIST_COLS], U16, name="buckets")
         bias_pool = keep.tile([P, U], F32, name="bias_pool")
         word_pool = keep.tile([P, T], U32, name="word_pool")
         byte_pool = keep.tile([P, T], U8, name="byte_pool")
@@ -56,17 +59,19 @@ def tile_attend_mixedbias_kernel(tc, query, keys_words, keys_scales, bias, gate,
             nc.sync.dma_start(val_pool[n][:], vals[n * P : (n + 1) * P, :])
             if n == 0:
                 nc.sync.dma_start(
-                    size_rows[0:2, :].rearrange("h (g r) -> h g r", r=RUN), size[0].rearrange("(g h r) -> h g r", h=2, r=RUN)
+                    size_rows[0:2, :].rearrange("h (g r) -> h g r", r=RUN),
+                    size[0].rearrange("(g h r) -> h g r", h=2, r=RUN),
                 )
 
         ident = keep.tile([P, P], F32, name="ident")
         make_identity(nc, ident[:])
 
+        halves = [slice(h * HALF, (h + 1) * HALF) for h in range(2)]
+        list_halves = [slice(h * LIST_COLS // 2, (h + 1) * LIST_COLS // 2) for h in range(2)]
+
         bias_g = keep.tile([P, I], F32, name="bias_g")
         for h in range(2):
-            nc.vector.tensor_copy(
-                bias_g[:, h * 256 : (h + 1) * 256], bias_pool[:].indirect(buckets[:, h * 16 : (h + 1) * 16])
-            )
+            nc.vector.tensor_copy(bias_g[:, halves[h]], bias_pool[:].indirect(buckets[:, list_halves[h]]))
 
         k_codes = keep.tile([P, I], U32, name="k_codes", align_bytes=64)
         k_scales = keep.tile([P, I], U8, name="k_scales", align_bytes=64)
@@ -77,10 +82,10 @@ def tile_attend_mixedbias_kernel(tc, query, keys_words, keys_scales, bias, gate,
         q_codes = keep.tile([P, Q], U32, name="q_codes", align_bytes=64)
         q_scales = keep.tile([P, Q], U8, name="q_scales", align_bytes=64)
         nc.vector.quantize_mx(q_codes[:].bitcast(FP8X4), q_scales[:], q_bf[:].rearrange("p q j -> p (q j)"))
-        halves = [slice(h * HALF, (h + 1) * HALF) for h in range(2)]
+
         scores = []
         for h in range(2):
-            nc.vector.tensor_copy(k_codes[:, halves[h]], word_pool[:].indirect(slots[:, h * 16 : (h + 1) * 16]))
+            nc.vector.tensor_copy(k_codes[:, halves[h]], word_pool[:].indirect(slots[:, list_halves[h]]))
             scores.append(psum.tile([P, HALF], F32, name="scores%d" % h))
             nc.tensor.matmul_mx(
                 scores[h][:],
@@ -100,19 +105,18 @@ def tile_attend_mixedbias_kernel(tc, query, keys_words, keys_scales, bias, gate,
             nc.tensor.transpose(size_turned[:, e, :], size_rows[:, e:HALF:2], ident[:])
         nc.scalar.copy(size_cols[:], size_turned[:, :, 0:2].rearrange("p e h -> p h e"))
 
-        def turn_pairs(rows_bf, grouped):
-            words = rows_bf[:].bitcast(F32)
-            turned = turn.tile([P, 2, P], F32, name="turned")
-            for u in range(2):
-                nc.tensor.transpose(turned[:, u, :], words[:, u * P : (u + 1) * P], ident[:])
-            nc.scalar.copy(
-                grouped.bitcast(F32).rearrange("p (x u) -> p x u", u=2), turned[:].rearrange("p u x -> p x u")
-            )
-
-        def gather_values(n, grouped, slot):
-            val_g = keep.tile([P, I], BF16, name="val_g%d" % n, tag=slot)
+        def gather_values(n, grouped, tag):
+            val_g = keep.tile([P, I], BF16, name="val_g%d" % n, tag=tag)
             nc.vector.tensor_copy(dealt(val_g), val_pool[n][:].indirect(slots[:]))
-            turn_pairs(val_g, grouped)
+            pairs = val_g[:].bitcast(F32)
+            turned = turn.tile([P, 2, P], F32, name="turned")
+            for h in range(2):
+                nc.tensor.transpose(turned[:, h, :], pairs[:, h * P : (h + 1) * P], ident[:])
+            grouped_pairs = grouped.bitcast(F32).rearrange("p (x h) -> p x h", h=2)
+            width = PIECE if n == E_TILES - 1 else P
+            for first in range(0, P, width):
+                cols = slice(first, first + width)
+                nc.scalar.copy(grouped_pairs[:, cols, :], turned[:].rearrange("p h x -> p x h")[:, cols, :])
 
         early_bf = keep.tile([P, E_TILES * I], BF16, name="early_bf", tag="val_pool2", align_bytes=64)
         late_bf = keep.tile([P, I], BF16, name="late_bf", align_bytes=64)
@@ -145,21 +149,23 @@ def tile_attend_mixedbias_kernel(tc, query, keys_words, keys_scales, bias, gate,
         gather_values(0, early_bf[:, I : 2 * I], "bias_g")
 
         inverse = keep.tile([P, 2], F32, name="inverse", align_bytes=64)
-        mix = keep.tile([P, 1], F32, name="mix")
+        factor_r = keep.tile([P, 1], F32, name="factor_r")
         nc.vector.reciprocal(inverse[:], sums[:])
         rest_col = keep.tile([P, 1], F32, name="rest_col", tag="q_raw")
         nc.scalar.activation(rest_col[:], gate_col[:], ACT.Copy, scale=-1.0, bias=1.0)
-        nc.scalar.activation(mix[:], inverse[:, 1:2], ACT.Copy, scale=rest_col[:])
+        nc.scalar.activation(factor_r[:], inverse[:, 1:2], ACT.Copy, scale=rest_col[:])
         part_r = keep.tile([P, I], F32, name="part_r")
         part_p = keep.tile([P, I], F32, name="part_p")
-        nc.scalar.activation(part_r[:], exp_r[:], ACT.Copy, scale=mix[:])
+        nc.scalar.activation(part_r[:], exp_r[:], ACT.Copy, scale=factor_r[:])
         nc.vector.tensor_scalar(part_p[:], exp_p[:], inverse[:, 0:1], gate_col[:], ALU.mult, ALU.mult)
+
         mixed = psum.tile([P, PACK, P], F32, name="mixed")
         for k, part in enumerate((part_p, part_r)):
             for t in range(PACK):
+                h, e = divmod(t, 2)
                 nc.tensor.matmul(
                     mixed[:, t, :],
-                    part[:, (t // 2) * HALF + t % 2 : (t // 2 + 1) * HALF : 2],
+                    part[:, h * HALF + e : (h + 1) * HALF : 2],
                     ident[:],
                     start=(k == 0 and t == 0),
                     stop=(k == 1 and t == PACK - 1),
@@ -178,18 +184,23 @@ def tile_attend_mixedbias_kernel(tc, query, keys_words, keys_scales, bias, gate,
 
         early_codes = keep.tile([P, E_TILES * P], U32, name="early_codes", tag="val_pool3", align_bytes=64)
         early_scales = keep.tile([P, E_TILES * P], U8, name="early_scales", align_bytes=64)
-        for h in range(2):
-            cols = slice(h * 2 * P, (h + 1) * 2 * P)
+        for c in range(2):
+            cols = slice(c * 2 * P, (c + 1) * 2 * P)
             nc.vector.quantize_mx(
-                early_codes[:, cols].bitcast(FP8X4), early_scales[:, cols], early_bf[:, h * 2 * I : (h + 1) * 2 * I]
+                early_codes[:, cols].bitcast(FP8X4), early_scales[:, cols], early_bf[:, c * 2 * I : (c + 1) * 2 * I]
             )
         late_codes = keep.tile([P, P], U32, name="late_codes", align_bytes=64)
         late_scales = keep.tile([P, P], U8, name="late_scales", align_bytes=64)
-        nc.vector.quantize_mx(late_codes[:].bitcast(FP8X4), late_scales[:], late_bf[:])
+        pieces = [slice(c * PIECE, (c + 1) * PIECE) for c in range(LAST_PIECES)]
+        for c, cols in enumerate(pieces):
+            nc.vector.quantize_mx(
+                late_codes[:, cols].bitcast(FP8X4),
+                late_scales[:, cols],
+                late_bf[:, c * PIECE * PACK : (c + 1) * PIECE * PACK],
+            )
 
-        def finish(name, codes, scales, first, copy, bank):
-            width = codes.shape[1]
-            acc = psum.tile([P, width], F32, name=name + "_acc", tag=bank)
+        def product(name, codes, scales, bank):
+            acc = psum.tile([P, codes.shape[1]], F32, name=name + "_acc", tag=bank)
             nc.tensor.matmul_mx(
                 acc[:],
                 lhsT=early_codes[:, 0:Q].bitcast(FP8X4),
@@ -199,10 +210,21 @@ def tile_attend_mixedbias_kernel(tc, query, keys_words, keys_scales, bias, gate,
                 start=True,
                 stop=True,
             )
-            result = keep.tile([P, width], F32, name=name + "_out")
-            copy(result[:], acc[:])
-            nc.sync.dma_start(out[:, first : first + width], result[:])
+            return acc
 
-        finish("early", early_codes[:, P : 2 * P], early_scales[:, P : 2 * P], 0, nc.scalar.copy, "scores0")
-        finish("mid", early_codes[:, 2 * P : 4 * P], early_scales[:, 2 * P : 4 * P], P, nc.scalar.copy, "mid_acc")
-        finish("late", late_codes[:], late_scales[:], 3 * P, nc.vector.tensor_copy, "late_acc")
+        early_out = keep.tile([P, 2 * P], F32, name="early_out")
+        mid_out = keep.tile([P, P], F32, name="mid_out")
+        late_out = keep.tile([P, P], F32, name="late_out")
+        accs = [
+            product("tile%d" % n, early_codes[:, (n + 1) * P : (n + 2) * P], early_scales[:, (n + 1) * P : (n + 2) * P], bank)
+            for n, bank in enumerate(("scores0", "scores1", "mid_acc"))
+        ]
+        nc.scalar.copy(early_out[:, 0:P], accs[0][:])
+        nc.vector.tensor_copy(early_out[:, P : 2 * P], accs[1][:])
+        nc.sync.dma_start(out[:, 0 : 2 * P], early_out[:])
+        nc.scalar.copy(mid_out[:], accs[2][:])
+        nc.sync.dma_start(out[:, 2 * P : 3 * P], mid_out[:])
+        for c, bank in enumerate(("late_acc", "mixed")):
+            acc = product("late%d" % c, late_codes[:, pieces[c]], late_scales[:, pieces[c]], bank)
+            nc.vector.tensor_copy(late_out[:, pieces[c]], acc[:])
+        nc.sync.dma_start(out[:, 3 * P : 4 * P], late_out[:])

@@ -40,14 +40,18 @@ def tile_attend_mixedbias_kernel(tc, query, keys_words, keys_scales, bias, gate,
         word_pool = keep.tile([P, T], U32, name="word_pool")
         byte_pool = keep.tile([P, T], U8, name="byte_pool")
         q_raw = keep.tile([P, PACK, Q], F32, name="q_raw")
+        gate_row = keep.tile([P, Q], F32, name="gate_row")
         gate_col = keep.tile([P, 1], F32, name="gate_col")
-        size_rows = keep.tile([P, HALF], F32, name="size_rows")
-        size_cols = keep.tile([P, 2, 2], F32, name="size_cols")
+        rest_col = keep.tile([P, 1], F32, name="rest_col")
+        size_raw = keep.tile([1, I], F32, name="size_raw")
+        size_row = keep.tile([P, PACK, P], F32, name="size_row")
+        size_cols = keep.tile([P, PACK], F32, name="size_cols")
         val_pool = [keep.tile([P, T], F32, name="val_pool%d" % n, align_bytes=64) for n in range(E_TILES)]
 
         nc.gpsimd.memset(byte_pool[:].bitcast(I32), 0)
-        nc.gpsimd.memset(size_rows[:], 0.0)
-        nc.gpsimd.dma_start(gate_col[:], gate)
+        nc.gpsimd.memset(gate_row[:], 0.0)
+        nc.gpsimd.dma_start(gate_row[0:1, :], gate.rearrange("q one -> one q"))
+        nc.gpsimd.memset(size_row[:], 0.0)
         nc.sync.dma_start(buckets[:], offs2)
         nc.sync.dma_start(bias_pool[:], bias)
         nc.sync.dma_start(slots[:], offs)
@@ -55,13 +59,9 @@ def tile_attend_mixedbias_kernel(tc, query, keys_words, keys_scales, bias, gate,
         for r in range(4):
             nc.sync.dma_start(byte_pool[r:P:32, :].bitcast(I32), keys_scales[0, r:16:4, :].bitcast(I32))
         nc.sync.dma_start(word_pool[:].bitcast(I32), keys_words[0].rearrange("p n t -> p (n t)").bitcast(I32))
+        nc.sync.dma_start(size_raw[:], size)
         for n in range(E_TILES):
             nc.sync.dma_start(val_pool[n][:], vals[n * P : (n + 1) * P, :])
-            if n == 0:
-                nc.sync.dma_start(
-                    size_rows[0:2, :].rearrange("h (g r) -> h g r", r=RUN),
-                    size[0].rearrange("(g h r) -> h g r", h=2, r=RUN),
-                )
 
         ident = keep.tile([P, P], F32, name="ident")
         make_identity(nc, ident[:])
@@ -100,10 +100,18 @@ def tile_attend_mixedbias_kernel(tc, query, keys_words, keys_scales, bias, gate,
         def dealt(tile):
             return tile[:].rearrange("p (h g r) -> p g h r", h=2, r=RUN)
 
-        size_turned = psum.tile([P, 2, P], F32, name="size_turned", tag="mixed")
-        for e in range(2):
-            nc.tensor.transpose(size_turned[:, e, :], size_rows[:, e:HALF:2], ident[:])
-        nc.scalar.copy(size_cols[:], size_turned[:, :, 0:2].rearrange("p e h -> p h e"))
+        nc.scalar.copy(
+            size_row[0:1].rearrange("p (h e) (g j) -> p h e g j", h=2, j=RUN // 2),
+            size_raw[:].rearrange("p (g h j e) -> p h e g j", h=2, j=RUN // 2, e=2),
+        )
+        size_turned = psum.tile([P, PACK, P], F32, name="size_turned", tag="mixed")
+        for t in range(PACK):
+            nc.tensor.transpose(size_turned[:, t, :], size_row[:, t, :], ident[:])
+        gate_turned = psum.tile([P, Q], F32, name="gate_turned", tag="late_acc")
+        nc.tensor.transpose(gate_turned[:], gate_row[:], ident[:])
+        nc.scalar.copy(size_cols[:], size_turned[:, :, 0])
+        nc.scalar.copy(gate_col[:], gate_turned[:, 0:1])
+        nc.scalar.activation(rest_col[:], gate_turned[:, 0:1], ACT.Copy, scale=-1.0, bias=1.0)
 
         def gather_values(n, grouped, tag):
             val_g = keep.tile([P, I], BF16, name="val_g%d" % n, tag=tag)
@@ -151,8 +159,6 @@ def tile_attend_mixedbias_kernel(tc, query, keys_words, keys_scales, bias, gate,
         inverse = keep.tile([P, 2], F32, name="inverse", align_bytes=64)
         factor_r = keep.tile([P, 1], F32, name="factor_r")
         nc.vector.reciprocal(inverse[:], sums[:])
-        rest_col = keep.tile([P, 1], F32, name="rest_col", tag="q_raw")
-        nc.scalar.activation(rest_col[:], gate_col[:], ACT.Copy, scale=-1.0, bias=1.0)
         nc.scalar.activation(factor_r[:], inverse[:, 1:2], ACT.Copy, scale=rest_col[:])
         part_r = keep.tile([P, I], F32, name="part_r")
         part_p = keep.tile([P, I], F32, name="part_p")
@@ -176,7 +182,7 @@ def tile_attend_mixedbias_kernel(tc, query, keys_words, keys_scales, bias, gate,
         nc.vector.tensor_tensor(
             early_bf[:, 0:I].rearrange("p (q t) -> p q t", t=PACK),
             mixed[:].rearrange("p t q -> p q t"),
-            size_cols[:].rearrange("p h e -> p (h e)").unsqueeze(1).to_broadcast([P, Q, PACK]),
+            size_cols[:].unsqueeze(1).to_broadcast([P, Q, PACK]),
             ALU.mult,
         )
         gather_values(2, early_bf[:, 3 * I : 4 * I], "val_g2")

@@ -61,12 +61,14 @@ def tile_attend_mixedbias_kernel(tc, query, keys_words, keys_scales, bias, gate,
         nc.sync.dma_start(word_pool[:].bitcast(I32), keys_words[0].rearrange("p n t -> p (n t)").bitcast(I32))
         nc.sync.dma_start(size_raw[:], size)
         for n in range(E_TILES):
-            nc.sync.dma_start(val_pool[n][:], vals[n * P : (n + 1) * P, :])
+            rows = (0, 2, 1, 3)[n] * P
+            nc.sync.dma_start(val_pool[n][:], vals[rows : rows + P, :])
 
         ident = keep.tile([P, P], F32, name="ident")
         make_identity(nc, ident[:])
 
         halves = [slice(h * HALF, (h + 1) * HALF) for h in range(2)]
+        blocks = [slice(c * 8, (c + 1) * 8) for c in range(2)]
         list_halves = [slice(h * LIST_COLS // 2, (h + 1) * LIST_COLS // 2) for h in range(2)]
 
         bias_g = keep.tile([P, I], F32, name="bias_g")
@@ -113,9 +115,10 @@ def tile_attend_mixedbias_kernel(tc, query, keys_words, keys_scales, bias, gate,
         nc.scalar.copy(gate_col[:], gate_turned[:, 0:1])
         nc.scalar.activation(rest_col[:], gate_turned[:, 0:1], ACT.Copy, scale=-1.0, bias=1.0)
 
-        def gather_values(n, grouped, tag):
-            val_g = keep.tile([P, I], BF16, name="val_g%d" % n, tag=tag)
-            nc.vector.tensor_copy(dealt(val_g), val_pool[n][:].indirect(slots[:]))
+        def gather_values(n):
+            nc.vector.tensor_copy(dealt(val_g[n]), val_pool[n][:].indirect(slots[:]))
+
+        def turn_values(n, val_g, grouped):
             pairs = val_g[:].bitcast(F32)
             turned = turn.tile([P, 2, P], F32, name="turned")
             for h in range(2):
@@ -126,75 +129,94 @@ def tile_attend_mixedbias_kernel(tc, query, keys_words, keys_scales, bias, gate,
                 cols = slice(first, first + width)
                 nc.scalar.copy(grouped_pairs[:, cols, :], turned[:].rearrange("p h x -> p x h")[:, cols, :])
 
-        early_bf = keep.tile([P, E_TILES * I], BF16, name="early_bf", tag="val_pool2", align_bytes=64)
+        w_bf = keep.tile([P, I], BF16, name="w_bf", align_bytes=64)
+        early_bf = keep.tile([P, 3 * I], BF16, name="early_bf", tag="val_pool1", align_bytes=64)
         late_bf = keep.tile([P, I], BF16, name="late_bf", align_bytes=64)
 
-        biased = keep.tile([P, I], F32, name="biased")
-        negated = keep.tile([P, I], F32, name="negated")
         first_min = keep.tile([P, 1], F32, name="first_min")
         neg_max_r = keep.tile([P, 1], F32, name="neg_max_r")
         neg_max_p = keep.tile([P, 1], F32, name="neg_max_p")
+        sum_r = keep.tile([P, 1], F32, name="sum_r")
+        val_g = [keep.tile([P, I], BF16, name="val_g%d" % n) for n in range(E_TILES)]
+        sum_p = val_g[0][:].bitcast(F32)[:, 0:1]
+
+        biased = keep.tile([P, I], F32, name="biased")
+        negated = keep.tile([P, I], F32, name="negated")
         exp_r = keep.tile([P, I], F32, name="exp_r")
         exp_p = keep.tile([P, I], F32, name="exp_p")
-        sums = keep.tile([P, 2], F32, name="sums")
-        nc.vector.tensor_scalar(negated[:, halves[0]], scores[0][:], -1.0, None, ALU.mult, ALU.min, accum_out=first_min[:])
-        for h in range(2):
-            nc.vector.tensor_tensor(biased[:, halves[h]], scores[h][:], bias_g[:, halves[h]], ALU.add)
+        score_runs = [scores[c][:].rearrange("p (g h r) -> p g h r", h=2, r=RUN) for c in range(2)]
         nc.vector.tensor_scalar(
-            negated[:, halves[1]], scores[1][:], -1.0, first_min[:], ALU.mult, ALU.min, accum_out=neg_max_r[:]
+            dealt(negated)[:, blocks[0]], score_runs[0], -1.0, None, ALU.mult, ALU.min, accum_out=first_min[:]
+        )
+        for c in range(2):
+            nc.vector.tensor_tensor(
+                dealt(biased)[:, blocks[c]],
+                score_runs[c],
+                bias_g[:, halves[c]].rearrange("p (g h r) -> p g h r", h=2, r=RUN),
+                ALU.add,
+            )
+        nc.vector.tensor_scalar(
+            dealt(negated)[:, blocks[1]], score_runs[1], -1.0, first_min[:], ALU.mult, ALU.min, accum_out=neg_max_r[:]
         )
         nc.vector.tensor_reduce(neg_max_p[:], biased[:], AXIS_X, ALU.max, negate=True)
-        for exps, source, sign, neg_max, column in ((exp_r, negated, -1.0, neg_max_r, 1), (exp_p, biased, 1.0, neg_max_p, 0)):
+        for exps, source, sign, neg_max, total in (
+            (exp_r, negated, -1.0, neg_max_r[:], sum_r[:]),
+            (exp_p, biased, 1.0, neg_max_p[:], sum_p),
+        ):
             nc.scalar.activation(
-                dealt(exps),
-                source[:].rearrange("p (g h r) -> p g h r", h=2, r=RUN),
+                exps[:].rearrange("p (h e x) -> p h e x", h=2, e=2),
+                source[:].rearrange("p (h x e) -> p h e x", h=2, e=2),
                 ACT.Exp,
-                bias=neg_max[:],
+                bias=neg_max,
                 scale=sign,
-                accum_out=sums[:, column : column + 1],
+                accum_out=total,
             )
 
-        gather_values(0, early_bf[:, I : 2 * I], "bias_g")
-
-        inverse = keep.tile([P, 2], F32, name="inverse", align_bytes=64)
-        factor_r = keep.tile([P, 1], F32, name="factor_r")
-        nc.vector.reciprocal(inverse[:], sums[:])
-        nc.scalar.activation(factor_r[:], inverse[:, 1:2], ACT.Copy, scale=rest_col[:])
         part_r = keep.tile([P, I], F32, name="part_r")
         part_p = keep.tile([P, I], F32, name="part_p")
-        nc.scalar.activation(part_r[:], exp_r[:], ACT.Copy, scale=factor_r[:])
-        nc.vector.tensor_scalar(part_p[:], exp_p[:], inverse[:, 0:1], gate_col[:], ALU.mult, ALU.mult)
+        for name, part, exps, total, share in (("r", part_r, exp_r, sum_r[:], rest_col), ("p", part_p, exp_p, sum_p, gate_col)):
+            inverse = keep.tile([P, 1], F32, name="inverse_" + name)
+            nc.vector.reciprocal(inverse[:], total)
+            nc.vector.tensor_scalar(part[:], exps[:], inverse[:], share[:], ALU.mult, ALU.mult)
+
+        val_bf = keep.tile([P, T], BF16, name="val_bf")
+        for first in range(0, T, I):
+            nc.scalar.copy(val_bf[:, first : first + I], val_pool[1][:, first : first + I])
+        nc.scalar.activation(dealt(val_g[1]), val_bf[:].indirect(slots[:]), ACT.Copy)
 
         mixed = psum.tile([P, PACK, P], F32, name="mixed")
-        for k, part in enumerate((part_p, part_r)):
+        for k, part in enumerate((part_r, part_p)):
             for t in range(PACK):
-                h, e = divmod(t, 2)
                 nc.tensor.matmul(
                     mixed[:, t, :],
-                    part[:, h * HALF + e : (h + 1) * HALF : 2],
+                    part[:, t * P : (t + 1) * P],
                     ident[:],
                     start=(k == 0 and t == 0),
                     stop=(k == 1 and t == PACK - 1),
                     is_transpose=True,
                 )
-
-        gather_values(1, early_bf[:, 2 * I : 3 * I], "val_g1")
+        gather_values(0)
         nc.vector.tensor_tensor(
-            early_bf[:, 0:I].rearrange("p (q t) -> p q t", t=PACK),
+            w_bf[:].rearrange("p (q t) -> p q t", t=PACK),
             mixed[:].rearrange("p t q -> p q t"),
             size_cols[:].unsqueeze(1).to_broadcast([P, Q, PACK]),
             ALU.mult,
         )
-        gather_values(2, early_bf[:, 3 * I : 4 * I], "val_g2")
-        gather_values(3, late_bf[:], "val_g3")
+        turn_values(0, val_g[0], early_bf[:, 0:I])
+        gather_values(2)
+        turn_values(2, val_g[2], early_bf[:, I : 2 * I])
+        turn_values(1, val_g[1], early_bf[:, 2 * I : 3 * I])
+        gather_values(3)
+        turn_values(3, val_g[3], late_bf[:])
 
         early_codes = keep.tile([P, E_TILES * P], U32, name="early_codes", tag="val_pool3", align_bytes=64)
         early_scales = keep.tile([P, E_TILES * P], U8, name="early_scales", align_bytes=64)
-        for c in range(2):
-            cols = slice(c * 2 * P, (c + 1) * 2 * P)
-            nc.vector.quantize_mx(
-                early_codes[:, cols].bitcast(FP8X4), early_scales[:, cols], early_bf[:, c * 2 * I : (c + 1) * 2 * I]
-            )
+        for cols, source in (
+            (slice(0, P), w_bf[:]),
+            (slice(P, 3 * P), early_bf[:, 0 : 2 * I]),
+            (slice(3 * P, 4 * P), early_bf[:, 2 * I : 3 * I]),
+        ):
+            nc.vector.quantize_mx(early_codes[:, cols].bitcast(FP8X4), early_scales[:, cols], source)
         late_codes = keep.tile([P, P], U32, name="late_codes", align_bytes=64)
         late_scales = keep.tile([P, P], U8, name="late_scales", align_bytes=64)
         pieces = [slice(c * PIECE, (c + 1) * PIECE) for c in range(LAST_PIECES)]
@@ -226,7 +248,7 @@ def tile_attend_mixedbias_kernel(tc, query, keys_words, keys_scales, bias, gate,
             for n, bank in enumerate(("scores0", "scores1", "mid_acc"))
         ]
         nc.scalar.copy(early_out[:, 0:P], accs[0][:])
-        nc.vector.tensor_copy(early_out[:, P : 2 * P], accs[1][:])
+        nc.scalar.copy(early_out[:, P : 2 * P], accs[1][:])
         nc.sync.dma_start(out[:, 0 : 2 * P], early_out[:])
         nc.scalar.copy(mid_out[:], accs[2][:])
         nc.sync.dma_start(out[:, 2 * P : 3 * P], mid_out[:])

@@ -36,9 +36,10 @@ def tile_attend_mixedbias_kernel(tc, query, keys_words, keys_scales, bias, gate,
 
         slots = keep.tile([P, LIST_COLS], U16, name="slots")
         buckets = keep.tile([P, LIST_COLS], U16, name="buckets")
-        bias_pool = keep.tile([P, U], F32, name="bias_pool")
+        bias_pool = keep.tile([P, U], F32, name="bias_pool", tag="val_pool1", align_bytes=64)
         word_pool = keep.tile([P, T], U32, name="word_pool")
         byte_pool = keep.tile([P, T], U8, name="byte_pool")
+        k_scales = keep.tile([P, I], U8, name="k_scales", align_bytes=64)
         q_raw = keep.tile([P, PACK, Q], F32, name="q_raw")
         gate_row = keep.tile([P, Q], F32, name="gate_row")
         gate_col = keep.tile([P, 1], F32, name="gate_col")
@@ -46,23 +47,24 @@ def tile_attend_mixedbias_kernel(tc, query, keys_words, keys_scales, bias, gate,
         size_raw = keep.tile([1, I], F32, name="size_raw")
         size_row = keep.tile([P, PACK, P], F32, name="size_row")
         size_cols = keep.tile([P, PACK], F32, name="size_cols")
-        val_pool = [keep.tile([P, T], F32, name="val_pool%d" % n, align_bytes=64) for n in range(E_TILES)]
 
         nc.gpsimd.memset(byte_pool[:].bitcast(I32), 0)
+        nc.gpsimd.memset(k_scales[:].bitcast(I32), 0)
         nc.gpsimd.memset(gate_row[:], 0.0)
         nc.gpsimd.dma_start(gate_row[0:1, :], gate.rearrange("q one -> one q"))
         nc.gpsimd.memset(size_row[:], 0.0)
+        nc.sync.dma_start(q_raw[:], query.rearrange("(p j) q -> p j q", j=PACK))
+        nc.sync.dma_start(slots[:], offs)
+        nc.sync.dma_start(byte_pool[0:P:8, :].bitcast(I32), keys_scales[0].bitcast(I32))
         nc.sync.dma_start(buckets[:], offs2)
         nc.sync.dma_start(bias_pool[:], bias)
-        nc.sync.dma_start(slots[:], offs)
-        nc.sync.dma_start(q_raw[:], query.rearrange("(p j) q -> p j q", j=PACK))
-        for r in range(4):
-            nc.sync.dma_start(byte_pool[r:P:32, :].bitcast(I32), keys_scales[0, r:16:4, :].bitcast(I32))
         nc.sync.dma_start(word_pool[:].bitcast(I32), keys_words[0].rearrange("p n t -> p (n t)").bitcast(I32))
         nc.sync.dma_start(size_raw[:], size)
-        for n in range(E_TILES):
-            rows = (0, 2, 1, 3)[n] * P
-            nc.sync.dma_start(val_pool[n][:], vals[rows : rows + P, :])
+
+        spread_scales = keep.tile([P, I], U8, name="spread_scales")
+        nc.vector.tensor_copy(spread_scales[:], byte_pool[:].indirect(slots[:]))
+        for r in range(4):
+            nc.scalar.dma_start(k_scales[r:P:32, :].bitcast(I32), spread_scales[8 * r : P : 32, :].bitcast(I32))
 
         ident = keep.tile([P, P], F32, name="ident")
         make_identity(nc, ident[:])
@@ -75,9 +77,12 @@ def tile_attend_mixedbias_kernel(tc, query, keys_words, keys_scales, bias, gate,
         for h in range(2):
             nc.vector.tensor_copy(bias_g[:, halves[h]], bias_pool[:].indirect(buckets[:, list_halves[h]]))
 
+        val_pool = [keep.tile([P, T], F32, name="val_pool%d" % n, align_bytes=64) for n in range(E_TILES)]
+        for n in range(E_TILES):
+            rows = (0, 2, 1, 3)[n] * P
+            nc.sync.dma_start(val_pool[n][:], vals[rows : rows + P, :])
+
         k_codes = keep.tile([P, I], U32, name="k_codes", align_bytes=64)
-        k_scales = keep.tile([P, I], U8, name="k_scales", align_bytes=64)
-        nc.vector.tensor_copy(k_scales[:], byte_pool[:].indirect(slots[:]))
 
         q_bf = keep.tile([P, Q, PACK], BF16, name="q_bf", align_bytes=64)
         nc.scalar.copy(q_bf[:], q_raw[:].rearrange("p j q -> p q j"))

@@ -36,9 +36,9 @@ def tile_attend_mixedbias_kernel(tc, query, keys_words, keys_scales, bias, gate,
 
         slots = keep.tile([P, LIST_COLS], U16, name="slots")
         buckets = keep.tile([P, LIST_COLS], U16, name="buckets")
-        bias_pool = keep.tile([P, U], F32, name="bias_pool", tag="val_pool1", align_bytes=64)
+        bias_pool = keep.tile([P, U], F32, name="bias_pool")
         word_pool = keep.tile([P, T], U32, name="word_pool")
-        byte_pool = keep.tile([P, T], U8, name="byte_pool")
+        byte_pool = keep.tile([P, T], U8, name="byte_pool", tag="val_pool0", align_bytes=64)
         k_scales = keep.tile([P, I], U8, name="k_scales", align_bytes=64)
         q_raw = keep.tile([P, PACK, Q], F32, name="q_raw")
         gate_row = keep.tile([P, Q], F32, name="gate_row")
@@ -60,11 +60,13 @@ def tile_attend_mixedbias_kernel(tc, query, keys_words, keys_scales, bias, gate,
         nc.sync.dma_start(bias_pool[:], bias)
         nc.sync.dma_start(word_pool[:].bitcast(I32), keys_words[0].rearrange("p n t -> p (n t)").bitcast(I32))
         nc.sync.dma_start(size_raw[:], size)
+        val_head = keep.tile([P, I], F32, name="val_head")
+        nc.sync.dma_start(val_head[:], vals[2 * P : 3 * P, 0:I])
 
         spread_scales = keep.tile([P, I], U8, name="spread_scales")
         nc.vector.tensor_copy(spread_scales[:], byte_pool[:].indirect(slots[:]))
         for r in range(4):
-            nc.scalar.dma_start(k_scales[r:P:32, :].bitcast(I32), spread_scales[8 * r : P : 32, :].bitcast(I32))
+            nc.sync.dma_start(k_scales[r:P:32, :].bitcast(I32), spread_scales[8 * r : P : 32, :].bitcast(I32))
 
         ident = keep.tile([P, P], F32, name="ident")
         make_identity(nc, ident[:])
@@ -78,9 +80,10 @@ def tile_attend_mixedbias_kernel(tc, query, keys_words, keys_scales, bias, gate,
             nc.vector.tensor_copy(bias_g[:, halves[h]], bias_pool[:].indirect(buckets[:, list_halves[h]]))
 
         val_pool = [keep.tile([P, T], F32, name="val_pool%d" % n, align_bytes=64) for n in range(E_TILES)]
-        for n in range(E_TILES):
-            rows = (0, 2, 1, 3)[n] * P
-            nc.sync.dma_start(val_pool[n][:], vals[rows : rows + P, :])
+        nc.sync.dma_start(val_pool[0][:], vals[0:P, :])
+        nc.sync.dma_start(val_pool[1][:, I:T], vals[2 * P : 3 * P, I:T])
+        nc.sync.dma_start(val_pool[2][:], vals[P : 2 * P, :])
+        nc.sync.dma_start(val_pool[3][:], vals[3 * P : 4 * P, :])
 
         k_codes = keep.tile([P, I], U32, name="k_codes", align_bytes=64)
 
@@ -185,7 +188,8 @@ def tile_attend_mixedbias_kernel(tc, query, keys_words, keys_scales, bias, gate,
             nc.vector.tensor_scalar(part[:], exps[:], inverse[:], share[:], ALU.mult, ALU.mult)
 
         val_bf = keep.tile([P, T], BF16, name="val_bf")
-        for first in range(0, T, I):
+        nc.scalar.copy(val_bf[:, 0:I], val_head[:])
+        for first in range(I, T, I):
             nc.scalar.copy(val_bf[:, first : first + I], val_pool[1][:, first : first + I])
         nc.scalar.activation(dealt(val_g[1]), val_bf[:].indirect(slots[:]), ACT.Copy)
 

@@ -38,7 +38,7 @@ def tile_attend_mixedbias_kernel(tc, query, keys_words, keys_scales, bias, gate,
         buckets = keep.tile([P, LIST_COLS], U16, name="buckets")
         bias_pool = keep.tile([P, U], F32, name="bias_pool")
         word_pool = keep.tile([P, T], U32, name="word_pool")
-        byte_pool = keep.tile([P, T], U8, name="byte_pool", tag="val_pool0", align_bytes=64)
+        byte_pool = keep.tile([P, T], U8, name="byte_pool", tag="val_pool1", align_bytes=64)
         k_scales = keep.tile([P, I], U8, name="k_scales", align_bytes=64)
         q_raw = keep.tile([P, PACK, Q], F32, name="q_raw")
         gate_row = keep.tile([P, Q], F32, name="gate_row")
@@ -46,7 +46,6 @@ def tile_attend_mixedbias_kernel(tc, query, keys_words, keys_scales, bias, gate,
         rest_col = keep.tile([P, 1], F32, name="rest_col")
         size_raw = keep.tile([1, I], F32, name="size_raw")
         size_row = keep.tile([P, PACK, P], F32, name="size_row")
-        size_cols = keep.tile([P, PACK], F32, name="size_cols")
 
         nc.gpsimd.memset(byte_pool[:].bitcast(I32), 0)
         nc.gpsimd.memset(k_scales[:].bitcast(I32), 0)
@@ -60,8 +59,8 @@ def tile_attend_mixedbias_kernel(tc, query, keys_words, keys_scales, bias, gate,
         nc.sync.dma_start(bias_pool[:], bias)
         nc.sync.dma_start(word_pool[:].bitcast(I32), keys_words[0].rearrange("p n t -> p (n t)").bitcast(I32))
         nc.sync.dma_start(size_raw[:], size)
-        val_head = keep.tile([P, I], F32, name="val_head")
-        nc.sync.dma_start(val_head[:], vals[2 * P : 3 * P, 0:I])
+        val_head = keep.tile([P, 2 * I], F32, name="val_head")
+        nc.sync.dma_start(val_head[:], vals[2 * P : 3 * P, 0 : 2 * I])
 
         spread_scales = keep.tile([P, I], U8, name="spread_scales")
         nc.vector.tensor_copy(spread_scales[:], byte_pool[:].indirect(slots[:]))
@@ -80,8 +79,8 @@ def tile_attend_mixedbias_kernel(tc, query, keys_words, keys_scales, bias, gate,
             nc.vector.tensor_copy(bias_g[:, halves[h]], bias_pool[:].indirect(buckets[:, list_halves[h]]))
 
         val_pool = [keep.tile([P, T], F32, name="val_pool%d" % n, align_bytes=64) for n in range(E_TILES)]
+        nc.sync.dma_start(val_pool[1][:, 2 * I : T], vals[2 * P : 3 * P, 2 * I : T])
         nc.sync.dma_start(val_pool[0][:], vals[0:P, :])
-        nc.sync.dma_start(val_pool[1][:, I:T], vals[2 * P : 3 * P, I:T])
         nc.sync.dma_start(val_pool[2][:], vals[P : 2 * P, :])
         nc.sync.dma_start(val_pool[3][:], vals[3 * P : 4 * P, :])
 
@@ -114,12 +113,8 @@ def tile_attend_mixedbias_kernel(tc, query, keys_words, keys_scales, bias, gate,
             size_row[0:1].rearrange("p (h e) (g j) -> p h e g j", h=2, j=RUN // 2),
             size_raw[:].rearrange("p (g h j e) -> p h e g j", h=2, j=RUN // 2, e=2),
         )
-        size_turned = psum.tile([P, PACK, P], F32, name="size_turned", tag="mixed")
-        for t in range(PACK):
-            nc.tensor.transpose(size_turned[:, t, :], size_row[:, t, :], ident[:])
         gate_turned = psum.tile([P, Q], F32, name="gate_turned", tag="late_acc")
         nc.tensor.transpose(gate_turned[:], gate_row[:], ident[:])
-        nc.scalar.copy(size_cols[:], size_turned[:, :, 0])
         nc.scalar.copy(gate_col[:], gate_turned[:, 0:1])
         nc.scalar.activation(rest_col[:], gate_turned[:, 0:1], ACT.Copy, scale=-1.0, bias=1.0)
 
@@ -137,21 +132,18 @@ def tile_attend_mixedbias_kernel(tc, query, keys_words, keys_scales, bias, gate,
                 cols = slice(first, first + width)
                 nc.scalar.copy(grouped_pairs[:, cols, :], turned[:].rearrange("p h x -> p x h")[:, cols, :])
 
-        w_bf = keep.tile([P, I], BF16, name="w_bf", align_bytes=64)
-        early_bf = keep.tile([P, 3 * I], BF16, name="early_bf", tag="val_pool1", align_bytes=64)
         late_bf = keep.tile([P, I], BF16, name="late_bf", align_bytes=64)
 
         first_min = keep.tile([P, 1], F32, name="first_min")
         neg_max_r = keep.tile([P, 1], F32, name="neg_max_r")
         neg_max_p = keep.tile([P, 1], F32, name="neg_max_p")
         sum_r = keep.tile([P, 1], F32, name="sum_r")
-        val_g = [keep.tile([P, I], BF16, name="val_g%d" % n) for n in range(E_TILES)]
-        sum_p = val_g[0][:].bitcast(F32)[:, 0:1]
-
         biased = keep.tile([P, I], F32, name="biased")
         negated = keep.tile([P, I], F32, name="negated")
         exp_r = keep.tile([P, I], F32, name="exp_r")
         exp_p = keep.tile([P, I], F32, name="exp_p")
+        val_g = [keep.tile([P, I], BF16, name="val_g%d" % n, tag="biased" if n == 1 else "val_g%d" % n) for n in range(E_TILES)]
+        sum_p = val_g[0][:].bitcast(F32)[:, 0:1]
         score_runs = [scores[c][:].rearrange("p (g h r) -> p g h r", h=2, r=RUN) for c in range(2)]
         nc.vector.tensor_scalar(
             dealt(negated)[:, blocks[0]], score_runs[0], -1.0, None, ALU.mult, ALU.min, accum_out=first_min[:]
@@ -167,6 +159,9 @@ def tile_attend_mixedbias_kernel(tc, query, keys_words, keys_scales, bias, gate,
             dealt(negated)[:, blocks[1]], score_runs[1], -1.0, first_min[:], ALU.mult, ALU.min, accum_out=neg_max_r[:]
         )
         nc.vector.tensor_reduce(neg_max_p[:], biased[:], AXIS_X, ALU.max, negate=True)
+        size_turned = psum.tile([P, PACK, P], F32, name="size_turned", tag="scores0")
+        for t in range(PACK):
+            nc.tensor.transpose(size_turned[:, t, :], size_row[:, t, :], ident[:])
         for exps, source, sign, neg_max, total in (
             (exp_r, negated, -1.0, neg_max_r[:], sum_r[:]),
             (exp_p, biased, 1.0, neg_max_p[:], sum_p),
@@ -180,6 +175,9 @@ def tile_attend_mixedbias_kernel(tc, query, keys_words, keys_scales, bias, gate,
                 accum_out=total,
             )
 
+        size_cols = keep.tile([P, PACK], F32, name="size_cols", tag="neg_max_p")
+        nc.scalar.copy(size_cols[:], size_turned[:, :, 0])
+
         part_r = keep.tile([P, I], F32, name="part_r")
         part_p = keep.tile([P, I], F32, name="part_p")
         for name, part, exps, total, share in (("r", part_r, exp_r, sum_r[:], rest_col), ("p", part_p, exp_p, sum_p, gate_col)):
@@ -187,9 +185,9 @@ def tile_attend_mixedbias_kernel(tc, query, keys_words, keys_scales, bias, gate,
             nc.vector.reciprocal(inverse[:], total)
             nc.vector.tensor_scalar(part[:], exps[:], inverse[:], share[:], ALU.mult, ALU.mult)
 
-        val_bf = keep.tile([P, T], BF16, name="val_bf")
-        nc.scalar.copy(val_bf[:, 0:I], val_head[:])
-        for first in range(I, T, I):
+        val_bf = keep.tile([P, T], BF16, name="val_bf", align_bytes=64)
+        nc.scalar.copy(val_bf[:, 0 : 2 * I], val_head[:])
+        for first in range(2 * I, T, I):
             nc.scalar.copy(val_bf[:, first : first + I], val_pool[1][:, first : first + I])
         nc.scalar.activation(dealt(val_g[1]), val_bf[:].indirect(slots[:]), ACT.Copy)
 
@@ -204,28 +202,25 @@ def tile_attend_mixedbias_kernel(tc, query, keys_words, keys_scales, bias, gate,
                     stop=(k == 1 and t == PACK - 1),
                     is_transpose=True,
                 )
+        early_bf = keep.tile([P, E_TILES * I], BF16, name="early_bf", tag="val_bf", align_bytes=64)
         gather_values(0)
-        nc.vector.tensor_tensor(
-            w_bf[:].rearrange("p (q t) -> p q t", t=PACK),
-            mixed[:].rearrange("p t q -> p q t"),
-            size_cols[:].unsqueeze(1).to_broadcast([P, Q, PACK]),
-            ALU.mult,
-        )
-        turn_values(0, val_g[0], early_bf[:, 0:I])
+        w_places = early_bf[:, 0:I].rearrange("p (q t) -> p t q", t=PACK)
+        for t in range(PACK):
+            nc.scalar.activation(w_places[:, t, :], mixed[:, t, :], ACT.Copy, scale=size_cols[:, t : t + 1])
+        turn_values(0, val_g[0], early_bf[:, I : 2 * I])
         gather_values(2)
-        turn_values(2, val_g[2], early_bf[:, I : 2 * I])
-        turn_values(1, val_g[1], early_bf[:, 2 * I : 3 * I])
+        turn_values(2, val_g[2], early_bf[:, 2 * I : 3 * I])
+        turn_values(1, val_g[1], early_bf[:, 3 * I : 4 * I])
         gather_values(3)
         turn_values(3, val_g[3], late_bf[:])
 
         early_codes = keep.tile([P, E_TILES * P], U32, name="early_codes", tag="val_pool3", align_bytes=64)
         early_scales = keep.tile([P, E_TILES * P], U8, name="early_scales", align_bytes=64)
-        for cols, source in (
-            (slice(0, P), w_bf[:]),
-            (slice(P, 3 * P), early_bf[:, 0 : 2 * I]),
-            (slice(3 * P, 4 * P), early_bf[:, 2 * I : 3 * I]),
-        ):
-            nc.vector.quantize_mx(early_codes[:, cols].bitcast(FP8X4), early_scales[:, cols], source)
+        for c in range(2):
+            cols = slice(c * 2 * P, (c + 1) * 2 * P)
+            nc.vector.quantize_mx(
+                early_codes[:, cols].bitcast(FP8X4), early_scales[:, cols], early_bf[:, c * 2 * I : (c + 1) * 2 * I]
+            )
         late_codes = keep.tile([P, P], U32, name="late_codes", align_bytes=64)
         late_scales = keep.tile([P, P], U8, name="late_scales", align_bytes=64)
         pieces = [slice(c * PIECE, (c + 1) * PIECE) for c in range(LAST_PIECES)]

@@ -23,6 +23,7 @@ E_TILES = E // P
 HALF = I // 2
 RUN = 16
 LIST_COLS = I // 16
+GATE_ROW = 32
 LAST_PIECES = 2
 PIECE = P // LAST_PIECES
 
@@ -31,35 +32,34 @@ def tile_attend_mixedbias_kernel(tc, query, keys_words, keys_scales, bias, gate,
     nc = tc.nc
     with ExitStack() as ctx:
         keep = ctx.enter_context(tc.tile_pool(name="keep", bufs=1))
+        placed = ctx.enter_context(tc.tile_pool(name="placed", bufs=1))
         psum = ctx.enter_context(tc.psum_pool(name="psum", bufs=1))
         turn = ctx.enter_context(tc.psum_pool(name="turn", bufs=3))
 
         slots = keep.tile([P, LIST_COLS], U16, name="slots")
         buckets = keep.tile([P, LIST_COLS], U16, name="buckets")
-        bias_pool = keep.tile([P, U], F32, name="bias_pool")
-        word_pool = keep.tile([P, T], U32, name="word_pool")
-        byte_pool = keep.tile([P, T], U8, name="byte_pool", tag="val_pool1", align_bytes=64)
+        bias_pool = keep.tile([P, U], F32, name="bias_pool", tag="val_pool0", align_bytes=64)
+        word_pool = keep.tile([P, T], U32, name="word_pool", tag="val_pool2", align_bytes=64)
+        byte_pool = placed.tile([P, T], U8, name="byte_pool", offset=0, align_bytes=64)
         k_scales = keep.tile([P, I], U8, name="k_scales", align_bytes=64)
         q_raw = keep.tile([P, PACK, Q], F32, name="q_raw")
-        gate_row = keep.tile([P, Q], F32, name="gate_row")
+        gate_raw = keep.tile([GATE_ROW + 1, Q], F32, name="gate_raw")
         gate_col = keep.tile([P, 1], F32, name="gate_col")
         rest_col = keep.tile([P, 1], F32, name="rest_col")
         size_raw = keep.tile([1, I], F32, name="size_raw")
-        size_row = keep.tile([P, PACK, P], F32, name="size_row")
+        size_cols = keep.tile([P, PACK], F32, name="size_cols")
 
         nc.gpsimd.memset(byte_pool[:].bitcast(I32), 0)
-        nc.gpsimd.memset(k_scales[:].bitcast(I32), 0)
-        nc.gpsimd.memset(gate_row[:], 0.0)
-        nc.gpsimd.dma_start(gate_row[0:1, :], gate.rearrange("q one -> one q"))
-        nc.gpsimd.memset(size_row[:], 0.0)
+        nc.vector.memset(k_scales[:].bitcast(I32), 0)
         nc.sync.dma_start(q_raw[:], query.rearrange("(p j) q -> p j q", j=PACK))
         nc.sync.dma_start(slots[:], offs)
-        nc.sync.dma_start(byte_pool[0:P:8, :].bitcast(I32), keys_scales[0].bitcast(I32))
         nc.sync.dma_start(buckets[:], offs2)
+        nc.sync.dma_start(size_raw[:], size)
+        nc.sync.dma_start(gate_raw[GATE_ROW:, :], gate.rearrange("q one -> one q"))
+        nc.sync.dma_start(byte_pool[0:P:8, :].bitcast(I32), keys_scales[0].bitcast(I32))
         nc.sync.dma_start(bias_pool[:], bias)
         nc.sync.dma_start(word_pool[:].bitcast(I32), keys_words[0].rearrange("p n t -> p (n t)").bitcast(I32))
-        nc.sync.dma_start(size_raw[:], size)
-        val_head = keep.tile([P, 2 * I], F32, name="val_head")
+        val_head = keep.tile([P, 2 * I], F32, name="val_head", tag="val_pool3", align_bytes=64)
         nc.sync.dma_start(val_head[:], vals[2 * P : 3 * P, 0 : 2 * I])
 
         spread_scales = keep.tile([P, I], U8, name="spread_scales")
@@ -78,19 +78,30 @@ def tile_attend_mixedbias_kernel(tc, query, keys_words, keys_scales, bias, gate,
         for h in range(2):
             nc.vector.tensor_copy(bias_g[:, halves[h]], bias_pool[:].indirect(buckets[:, list_halves[h]]))
 
-        val_pool = [keep.tile([P, T], F32, name="val_pool%d" % n, align_bytes=64) for n in range(E_TILES)]
-        nc.sync.dma_start(val_pool[1][:, 2 * I : T], vals[2 * P : 3 * P, 2 * I : T])
+        val_pool = {n: keep.tile([P, T], F32, name="val_pool%d" % n, align_bytes=64) for n in (0, 2, 3)}
+        val_rest = placed.tile([P, 2 * I], F32, name="val_rest", offset=T // 2, align_bytes=64)
+        nc.sync.dma_start(val_rest[:], vals[2 * P : 3 * P, 2 * I : T])
         nc.sync.dma_start(val_pool[0][:], vals[0:P, :])
-        nc.sync.dma_start(val_pool[2][:], vals[P : 2 * P, :])
-        nc.sync.dma_start(val_pool[3][:], vals[3 * P : 4 * P, :])
 
         k_codes = keep.tile([P, I], U32, name="k_codes", align_bytes=64)
 
         q_bf = keep.tile([P, Q, PACK], BF16, name="q_bf", align_bytes=64)
         nc.scalar.copy(q_bf[:], q_raw[:].rearrange("p j q -> p q j"))
         q_codes = keep.tile([P, Q], U32, name="q_codes", align_bytes=64)
-        q_scales = keep.tile([P, Q], U8, name="q_scales", align_bytes=64)
+        q_scales = placed.tile([P, Q], U8, name="q_scales", offset=0, align_bytes=64)
         nc.vector.quantize_mx(q_codes[:].bitcast(FP8X4), q_scales[:], q_bf[:].rearrange("p q j -> p (q j)"))
+
+        nc.scalar.copy(
+            q_raw[0:1].rearrange("p (h e) (g j) -> p h e g j", h=2, j=RUN // 2),
+            size_raw[:].rearrange("p (g h j e) -> p h e g j", h=2, j=RUN // 2, e=2),
+        )
+        nc.scalar.copy(q_raw[GATE_ROW : GATE_ROW + 1, 0, :], gate_raw[GATE_ROW:, :])
+        rows_turned = psum.tile([P, PACK, P], F32, name="rows_turned", tag="mixed")
+        for t in range(PACK):
+            nc.tensor.transpose(rows_turned[:, t, :], q_raw[:, t, :], ident[:])
+        nc.scalar.copy(size_cols[:], rows_turned[:, :, 0])
+        nc.scalar.copy(gate_col[:], rows_turned[:, 0, GATE_ROW : GATE_ROW + 1])
+        nc.scalar.activation(rest_col[:], rows_turned[:, 0, GATE_ROW : GATE_ROW + 1], ACT.Copy, scale=-1.0, bias=1.0)
 
         scores = []
         for h in range(2):
@@ -106,17 +117,13 @@ def tile_attend_mixedbias_kernel(tc, query, keys_words, keys_scales, bias, gate,
                 stop=True,
             )
 
+        nc.sync.dma_start(val_pool[2][:], vals[P : 2 * P, :])
+        val_bf = keep.tile([P, T], BF16, name="val_bf", align_bytes=64)
+        nc.scalar.copy(val_bf[:, 0 : 2 * I], val_head[:])
+        nc.sync.dma_start(val_pool[3][:], vals[3 * P : 4 * P, :])
+
         def dealt(tile):
             return tile[:].rearrange("p (h g r) -> p g h r", h=2, r=RUN)
-
-        nc.scalar.copy(
-            size_row[0:1].rearrange("p (h e) (g j) -> p h e g j", h=2, j=RUN // 2),
-            size_raw[:].rearrange("p (g h j e) -> p h e g j", h=2, j=RUN // 2, e=2),
-        )
-        gate_turned = psum.tile([P, Q], F32, name="gate_turned", tag="late_acc")
-        nc.tensor.transpose(gate_turned[:], gate_row[:], ident[:])
-        nc.scalar.copy(gate_col[:], gate_turned[:, 0:1])
-        nc.scalar.activation(rest_col[:], gate_turned[:, 0:1], ACT.Copy, scale=-1.0, bias=1.0)
 
         def gather_values(n):
             nc.vector.tensor_copy(dealt(val_g[n]), val_pool[n][:].indirect(slots[:]))
@@ -136,14 +143,14 @@ def tile_attend_mixedbias_kernel(tc, query, keys_words, keys_scales, bias, gate,
 
         first_min = keep.tile([P, 1], F32, name="first_min")
         neg_max_r = keep.tile([P, 1], F32, name="neg_max_r")
-        neg_max_p = keep.tile([P, 1], F32, name="neg_max_p")
         sum_r = keep.tile([P, 1], F32, name="sum_r")
         biased = keep.tile([P, I], F32, name="biased")
         negated = keep.tile([P, I], F32, name="negated")
         exp_r = keep.tile([P, I], F32, name="exp_r")
         exp_p = keep.tile([P, I], F32, name="exp_p")
         val_g = [keep.tile([P, I], BF16, name="val_g%d" % n, tag="biased" if n == 1 else "val_g%d" % n) for n in range(E_TILES)]
-        sum_p = val_g[0][:].bitcast(F32)[:, 0:1]
+        neg_max_p = val_g[0][:].bitcast(F32)[:, 0:1]
+        sum_p = val_g[0][:].bitcast(F32)[:, HALF - 1 : HALF]
         score_runs = [scores[c][:].rearrange("p (g h r) -> p g h r", h=2, r=RUN) for c in range(2)]
         nc.vector.tensor_scalar(
             dealt(negated)[:, blocks[0]], score_runs[0], -1.0, None, ALU.mult, ALU.min, accum_out=first_min[:]
@@ -158,13 +165,10 @@ def tile_attend_mixedbias_kernel(tc, query, keys_words, keys_scales, bias, gate,
         nc.vector.tensor_scalar(
             dealt(negated)[:, blocks[1]], score_runs[1], -1.0, first_min[:], ALU.mult, ALU.min, accum_out=neg_max_r[:]
         )
-        nc.vector.tensor_reduce(neg_max_p[:], biased[:], AXIS_X, ALU.max, negate=True)
-        size_turned = psum.tile([P, PACK, P], F32, name="size_turned", tag="scores0")
-        for t in range(PACK):
-            nc.tensor.transpose(size_turned[:, t, :], size_row[:, t, :], ident[:])
+        nc.vector.tensor_reduce(neg_max_p, biased[:], AXIS_X, ALU.max, negate=True)
         for exps, source, sign, neg_max, total in (
             (exp_r, negated, -1.0, neg_max_r[:], sum_r[:]),
-            (exp_p, biased, 1.0, neg_max_p[:], sum_p),
+            (exp_p, biased, 1.0, neg_max_p, sum_p),
         ):
             nc.scalar.activation(
                 exps[:].rearrange("p (h e x) -> p h e x", h=2, e=2),
@@ -175,8 +179,6 @@ def tile_attend_mixedbias_kernel(tc, query, keys_words, keys_scales, bias, gate,
                 accum_out=total,
             )
 
-        size_cols = keep.tile([P, PACK], F32, name="size_cols", tag="neg_max_p")
-        nc.scalar.copy(size_cols[:], size_turned[:, :, 0])
 
         part_r = keep.tile([P, I], F32, name="part_r")
         part_p = keep.tile([P, I], F32, name="part_p")
@@ -185,10 +187,8 @@ def tile_attend_mixedbias_kernel(tc, query, keys_words, keys_scales, bias, gate,
             nc.vector.reciprocal(inverse[:], total)
             nc.vector.tensor_scalar(part[:], exps[:], inverse[:], share[:], ALU.mult, ALU.mult)
 
-        val_bf = keep.tile([P, T], BF16, name="val_bf", align_bytes=64)
-        nc.scalar.copy(val_bf[:, 0 : 2 * I], val_head[:])
-        for first in range(2 * I, T, I):
-            nc.scalar.copy(val_bf[:, first : first + I], val_pool[1][:, first : first + I])
+        for first in range(0, 2 * I, I):
+            nc.scalar.copy(val_bf[:, 2 * I + first : 3 * I + first], val_rest[:, first : first + I])
         nc.scalar.activation(dealt(val_g[1]), val_bf[:].indirect(slots[:]), ACT.Copy)
 
         mixed = psum.tile([P, PACK, P], F32, name="mixed")
@@ -203,7 +203,8 @@ def tile_attend_mixedbias_kernel(tc, query, keys_words, keys_scales, bias, gate,
                     is_transpose=True,
                 )
         early_bf = keep.tile([P, E_TILES * I], BF16, name="early_bf", tag="val_bf", align_bytes=64)
-        gather_values(0)
+        for c in range(2):
+            nc.vector.tensor_copy(dealt(val_g[0])[:, blocks[c]], val_pool[0][:].indirect(slots[:, list_halves[c]]))
         w_places = early_bf[:, 0:I].rearrange("p (q t) -> p t q", t=PACK)
         for t in range(PACK):
             nc.scalar.activation(w_places[:, t, :], mixed[:, t, :], ACT.Copy, scale=size_cols[:, t : t + 1])

@@ -23,6 +23,7 @@ E_TILES = E // P
 HALF = I // 2
 RUN = 16
 LIST_COLS = I // 16
+HEAD = 1152
 GATE_ROW = 32
 LAST_PIECES = 2
 PIECE = P // LAST_PIECES
@@ -59,8 +60,8 @@ def tile_attend_mixedbias_kernel(tc, query, keys_words, keys_scales, bias, gate,
         nc.sync.dma_start(byte_pool[0:P:8, :].bitcast(I32), keys_scales[0].bitcast(I32))
         nc.sync.dma_start(bias_pool[:], bias)
         nc.sync.dma_start(word_pool[:].bitcast(I32), keys_words[0].rearrange("p n t -> p (n t)").bitcast(I32))
-        val_head = keep.tile([P, 2 * I], F32, name="val_head", tag="val_pool3", align_bytes=64)
-        nc.sync.dma_start(val_head[:], vals[2 * P : 3 * P, 0 : 2 * I])
+        val_head = keep.tile([P, HEAD], F32, name="val_head", tag="val_pool3", align_bytes=64)
+        nc.sync.dma_start(val_head[:], vals[2 * P : 3 * P, 0:HEAD])
 
         spread_scales = keep.tile([P, I], U8, name="spread_scales")
         nc.vector.tensor_copy(spread_scales[:], byte_pool[:].indirect(slots[:]))
@@ -79,8 +80,8 @@ def tile_attend_mixedbias_kernel(tc, query, keys_words, keys_scales, bias, gate,
             nc.vector.tensor_copy(bias_g[:, halves[h]], bias_pool[:].indirect(buckets[:, list_halves[h]]))
 
         val_pool = {n: keep.tile([P, T], F32, name="val_pool%d" % n, align_bytes=64) for n in (0, 2, 3)}
-        val_rest = placed.tile([P, 2 * I], F32, name="val_rest", offset=T // 2, align_bytes=64)
-        nc.sync.dma_start(val_rest[:], vals[2 * P : 3 * P, 2 * I : T])
+        val_rest = placed.tile([P, T - HEAD], F32, name="val_rest", offset=T // 2, align_bytes=64)
+        nc.sync.dma_start(val_rest[:], vals[2 * P : 3 * P, HEAD:T])
         nc.sync.dma_start(val_pool[0][:], vals[0:P, :])
 
         k_codes = keep.tile([P, I], U32, name="k_codes", align_bytes=64)
@@ -119,7 +120,7 @@ def tile_attend_mixedbias_kernel(tc, query, keys_words, keys_scales, bias, gate,
 
         nc.sync.dma_start(val_pool[2][:], vals[P : 2 * P, :])
         val_bf = keep.tile([P, T], BF16, name="val_bf", align_bytes=64)
-        nc.scalar.copy(val_bf[:, 0 : 2 * I], val_head[:])
+        nc.scalar.copy(val_bf[:, 0:HEAD], val_head[:])
         nc.sync.dma_start(val_pool[3][:], vals[3 * P : 4 * P, :])
 
         def dealt(tile):
@@ -187,8 +188,9 @@ def tile_attend_mixedbias_kernel(tc, query, keys_words, keys_scales, bias, gate,
             nc.vector.reciprocal(inverse[:], total)
             nc.vector.tensor_scalar(part[:], exps[:], inverse[:], share[:], ALU.mult, ALU.mult)
 
-        for first in range(0, 2 * I, I):
-            nc.scalar.copy(val_bf[:, 2 * I + first : 3 * I + first], val_rest[:, first : first + I])
+        rest_half = (T - HEAD) // 2
+        for first in range(0, T - HEAD, rest_half):
+            nc.scalar.copy(val_bf[:, HEAD + first : HEAD + first + rest_half], val_rest[:, first : first + rest_half])
         nc.scalar.activation(dealt(val_g[1]), val_bf[:].indirect(slots[:]), ACT.Copy)
 
         mixed = psum.tile([P, PACK, P], F32, name="mixed")
@@ -205,9 +207,10 @@ def tile_attend_mixedbias_kernel(tc, query, keys_words, keys_scales, bias, gate,
         early_bf = keep.tile([P, E_TILES * I], BF16, name="early_bf", tag="val_bf", align_bytes=64)
         for c in range(2):
             nc.vector.tensor_copy(dealt(val_g[0])[:, blocks[c]], val_pool[0][:].indirect(slots[:, list_halves[c]]))
-        w_places = early_bf[:, 0:I].rearrange("p (q t) -> p t q", t=PACK)
+        w_places = keep.tile([P, PACK, Q], BF16, name="w_places")
         for t in range(PACK):
             nc.scalar.activation(w_places[:, t, :], mixed[:, t, :], ACT.Copy, scale=size_cols[:, t : t + 1])
+        nc.scalar.copy(early_bf[:, 0:I].rearrange("p (q t) -> p q t", t=PACK), w_places[:].rearrange("p t q -> p q t"))
         turn_values(0, val_g[0], early_bf[:, I : 2 * I])
         gather_values(2)
         turn_values(2, val_g[2], early_bf[:, 2 * I : 3 * I])

@@ -61,7 +61,7 @@ def tile_attend_mixedbias_kernel(tc, query, keys_words, keys_scales, bias, gate,
         nc.sync.dma_start(bias_pool[:], bias)
         nc.sync.dma_start(word_pool[:].bitcast(I32), keys_words[0].rearrange("p n t -> p (n t)").bitcast(I32))
         val_head = keep.tile([P, HEAD], F32, name="val_head", tag="val_pool3", align_bytes=64)
-        nc.sync.dma_start(val_head[:], vals[2 * P : 3 * P, 0:HEAD])
+        nc.sync.dma_start(val_head[:], vals[P : 2 * P, 0:HEAD])
 
         spread_scales = keep.tile([P, I], U8, name="spread_scales")
         nc.vector.tensor_copy(spread_scales[:], byte_pool[:].indirect(slots[:]))
@@ -81,7 +81,7 @@ def tile_attend_mixedbias_kernel(tc, query, keys_words, keys_scales, bias, gate,
 
         val_pool = {n: keep.tile([P, T], F32, name="val_pool%d" % n, align_bytes=64) for n in (0, 2, 3)}
         val_rest = placed.tile([P, T - HEAD], F32, name="val_rest", offset=T // 2, align_bytes=64)
-        nc.sync.dma_start(val_rest[:], vals[2 * P : 3 * P, HEAD:T])
+        nc.sync.dma_start(val_rest[:], vals[P : 2 * P, HEAD:T])
         nc.sync.dma_start(val_pool[0][:], vals[0:P, :])
 
         k_codes = keep.tile([P, I], U32, name="k_codes", align_bytes=64)
@@ -118,7 +118,7 @@ def tile_attend_mixedbias_kernel(tc, query, keys_words, keys_scales, bias, gate,
                 stop=True,
             )
 
-        nc.sync.dma_start(val_pool[2][:], vals[P : 2 * P, :])
+        nc.sync.dma_start(val_pool[2][:], vals[2 * P : 3 * P, :])
         val_bf = keep.tile([P, T], BF16, name="val_bf", align_bytes=64)
         nc.scalar.copy(val_bf[:, 0:HEAD], val_head[:])
         nc.sync.dma_start(val_pool[3][:], vals[3 * P : 4 * P, :])
@@ -149,7 +149,10 @@ def tile_attend_mixedbias_kernel(tc, query, keys_words, keys_scales, bias, gate,
         negated = keep.tile([P, I], F32, name="negated")
         exp_r = keep.tile([P, I], F32, name="exp_r")
         exp_p = keep.tile([P, I], F32, name="exp_p")
-        val_g = [keep.tile([P, I], BF16, name="val_g%d" % n, tag="biased" if n == 1 else "val_g%d" % n) for n in range(E_TILES)]
+        places_and_first = keep.tile([P, HALF + I], BF16, name="places_and_first")
+        w_places = places_and_first[:, 0:I].rearrange("p (t q) -> p t q", t=PACK)
+        val_g = [places_and_first[:, HALF:]]
+        val_g.extend(keep.tile([P, I], BF16, name="val_g%d" % n, tag=tag) for n, tag in ((1, "biased"), (2, "val_g2"), (3, "val_g3")))
         neg_max_p = val_g[0][:].bitcast(F32)[:, 0:1]
         sum_p = val_g[0][:].bitcast(F32)[:, HALF - 1 : HALF]
         score_runs = [scores[c][:].rearrange("p (g h r) -> p g h r", h=2, r=RUN) for c in range(2)]
@@ -207,24 +210,25 @@ def tile_attend_mixedbias_kernel(tc, query, keys_words, keys_scales, bias, gate,
         early_bf = keep.tile([P, E_TILES * I], BF16, name="early_bf", tag="val_bf", align_bytes=64)
         for c in range(2):
             nc.vector.tensor_copy(dealt(val_g[0])[:, blocks[c]], val_pool[0][:].indirect(slots[:, list_halves[c]]))
-        w_places = keep.tile([P, PACK, Q], BF16, name="w_places")
         for t in range(PACK):
+            if t == PACK // 2:
+                turn_values(1, val_g[1], early_bf[:, I : 2 * I])
+                turn_values(0, val_g[0], early_bf[:, 0:I])
             nc.scalar.activation(w_places[:, t, :], mixed[:, t, :], ACT.Copy, scale=size_cols[:, t : t + 1])
-        nc.scalar.copy(early_bf[:, 0:I].rearrange("p (q t) -> p q t", t=PACK), w_places[:].rearrange("p t q -> p q t"))
-        turn_values(0, val_g[0], early_bf[:, I : 2 * I])
+        nc.scalar.copy(
+            early_bf[:, 2 * I : 3 * I].rearrange("p (q t) -> p q t", t=PACK), w_places.rearrange("p t q -> p q t")
+        )
         gather_values(2)
-        turn_values(2, val_g[2], early_bf[:, 2 * I : 3 * I])
-        turn_values(1, val_g[1], early_bf[:, 3 * I : 4 * I])
+        first_codes = keep.tile([P, 2 * P], U32, name="first_codes", tag="val_pool2", align_bytes=64)
+        first_scales = keep.tile([P, 2 * P], U8, name="first_scales", align_bytes=64)
+        nc.vector.quantize_mx(first_codes[:].bitcast(FP8X4), first_scales[:], early_bf[:, 0 : 2 * I])
+        turn_values(2, val_g[2], early_bf[:, 3 * I : 4 * I])
         gather_values(3)
         turn_values(3, val_g[3], late_bf[:])
 
-        early_codes = keep.tile([P, E_TILES * P], U32, name="early_codes", tag="val_pool3", align_bytes=64)
-        early_scales = keep.tile([P, E_TILES * P], U8, name="early_scales", align_bytes=64)
-        for c in range(2):
-            cols = slice(c * 2 * P, (c + 1) * 2 * P)
-            nc.vector.quantize_mx(
-                early_codes[:, cols].bitcast(FP8X4), early_scales[:, cols], early_bf[:, c * 2 * I : (c + 1) * 2 * I]
-            )
+        early_codes = keep.tile([P, 2 * P], U32, name="early_codes", tag="val_pool3", align_bytes=64)
+        early_scales = keep.tile([P, 2 * P], U8, name="early_scales", align_bytes=64)
+        nc.vector.quantize_mx(early_codes[:].bitcast(FP8X4), early_scales[:], early_bf[:, 2 * I : 4 * I])
         late_codes = keep.tile([P, P], U32, name="late_codes", align_bytes=64)
         late_scales = keep.tile([P, P], U8, name="late_scales", align_bytes=64)
         pieces = [slice(c * PIECE, (c + 1) * PIECE) for c in range(LAST_PIECES)]
@@ -251,14 +255,11 @@ def tile_attend_mixedbias_kernel(tc, query, keys_words, keys_scales, bias, gate,
         early_out = keep.tile([P, 2 * P], F32, name="early_out")
         mid_out = keep.tile([P, P], F32, name="mid_out")
         late_out = keep.tile([P, P], F32, name="late_out")
-        accs = [
-            product("tile%d" % n, early_codes[:, (n + 1) * P : (n + 2) * P], early_scales[:, (n + 1) * P : (n + 2) * P], bank)
-            for n, bank in enumerate(("scores0", "scores1", "mid_acc"))
-        ]
-        nc.scalar.copy(early_out[:, 0:P], accs[0][:])
-        nc.scalar.copy(early_out[:, P : 2 * P], accs[1][:])
+        first_acc = product("first", first_codes[:], first_scales[:], "scores0")
+        mid_acc = product("mid", early_codes[:, P : 2 * P], early_scales[:, P : 2 * P], "mid_acc")
+        nc.scalar.copy(early_out[:], first_acc[:])
         nc.sync.dma_start(out[:, 0 : 2 * P], early_out[:])
-        nc.scalar.copy(mid_out[:], accs[2][:])
+        nc.scalar.copy(mid_out[:], mid_acc[:])
         nc.sync.dma_start(out[:, 2 * P : 3 * P], mid_out[:])
         for c, bank in enumerate(("late_acc", "mixed")):
             acc = product("late%d" % c, late_codes[:, pieces[c]], late_scales[:, pieces[c]], bank)

@@ -21,12 +21,14 @@ P = 128
 PACK = 4
 E_TILES = E // P
 HALF = I // 2
-RUN = 16
 LIST_COLS = I // 16
-HEAD = 1152
+SCALE_ROWS = D // 32
+ROW0 = P - SCALE_ROWS
 GATE_ROW = 32
 LAST_PIECES = 2
 PIECE = P // LAST_PIECES
+POOL_BYTES = 4 * T
+VECTOR_COLS = 16
 
 
 def tile_attend_mixedbias_kernel(tc, query, keys_words, keys_scales, bias, gate, size, vals, offs, offs2, out):
@@ -35,13 +37,13 @@ def tile_attend_mixedbias_kernel(tc, query, keys_words, keys_scales, bias, gate,
         keep = ctx.enter_context(tc.tile_pool(name="keep", bufs=1))
         placed = ctx.enter_context(tc.tile_pool(name="placed", bufs=1))
         psum = ctx.enter_context(tc.psum_pool(name="psum", bufs=1))
-        turn = ctx.enter_context(tc.psum_pool(name="turn", bufs=3))
+        turn = ctx.enter_context(tc.psum_pool(name="turn", bufs=2))
 
         slots = keep.tile([P, LIST_COLS], U16, name="slots")
         buckets = keep.tile([P, LIST_COLS], U16, name="buckets")
-        bias_pool = keep.tile([P, U], F32, name="bias_pool", tag="val_pool0", align_bytes=64)
-        word_pool = keep.tile([P, T], U32, name="word_pool", tag="val_pool2", align_bytes=64)
-        byte_pool = placed.tile([P, T], U8, name="byte_pool", offset=0, align_bytes=64)
+        bias_pool = keep.tile([P, U], F32, name="bias_pool", align_bytes=64)
+        word_pool = keep.tile([P, T], U32, name="word_pool", align_bytes=64)
+        byte_pool = keep.tile([P, T], U8, name="byte_pool", align_bytes=64)
         k_scales = keep.tile([P, I], U8, name="k_scales", align_bytes=64)
         q_raw = keep.tile([P, PACK, Q], F32, name="q_raw")
         gate_raw = keep.tile([GATE_ROW + 1, Q], F32, name="gate_raw")
@@ -49,53 +51,39 @@ def tile_attend_mixedbias_kernel(tc, query, keys_words, keys_scales, bias, gate,
         rest_col = keep.tile([P, 1], F32, name="rest_col")
         size_raw = keep.tile([1, I], F32, name="size_raw")
         size_cols = keep.tile([P, PACK], F32, name="size_cols")
+        val_pool = [placed.tile([P, T], F32, name="val_pool%d" % n, offset=n * POOL_BYTES, align_bytes=64) for n in range(E_TILES)]
 
-        nc.gpsimd.memset(byte_pool[:].bitcast(I32), 0)
+        nc.gpsimd.memset(byte_pool[0:ROW0, :].bitcast(I32), 0)
         nc.vector.memset(k_scales[:].bitcast(I32), 0)
-        nc.sync.dma_start(q_raw[:], query.rearrange("(p j) q -> p j q", j=PACK))
+        nc.sync.dma_start(byte_pool[ROW0:P, :].bitcast(I32), keys_scales[0].bitcast(I32))
+        nc.scalar.dma_start(q_raw[:], query.rearrange("(p j) q -> p j q", j=PACK))
         nc.sync.dma_start(slots[:], offs)
+        nc.scalar.dma_start(gate_raw[GATE_ROW:, :], gate.rearrange("q one -> one q"))
         nc.sync.dma_start(buckets[:], offs2)
-        nc.sync.dma_start(size_raw[:], size)
-        nc.sync.dma_start(gate_raw[GATE_ROW:, :], gate.rearrange("q one -> one q"))
-        nc.sync.dma_start(byte_pool[0:P:8, :].bitcast(I32), keys_scales[0].bitcast(I32))
-        nc.sync.dma_start(bias_pool[:], bias)
+        nc.scalar.dma_start(size_raw[:], size)
         nc.sync.dma_start(word_pool[:].bitcast(I32), keys_words[0].rearrange("p n t -> p (n t)").bitcast(I32))
-        val_head = keep.tile([P, HEAD], F32, name="val_head", tag="val_pool3", align_bytes=64)
-        nc.sync.dma_start(val_head[:], vals[P : 2 * P, 0:HEAD])
+        nc.sync.dma_start(bias_pool[:], bias)
 
-        spread_scales = keep.tile([P, I], U8, name="spread_scales")
-        nc.vector.tensor_copy(spread_scales[:], byte_pool[:].indirect(slots[:]))
+        row_scales = keep.tile([P, I], U8, name="row_scales")
+        nc.vector.tensor_copy(row_scales[:], byte_pool[:].indirect(slots[:]))
         for r in range(4):
-            nc.sync.dma_start(k_scales[r:P:32, :].bitcast(I32), spread_scales[8 * r : P : 32, :].bitcast(I32))
+            nc.sync.dma_start(k_scales[r:P:32, :].bitcast(I32), row_scales[ROW0 + r : P : 4, :].bitcast(I32))
+        for n in range(E_TILES):
+            nc.sync.dma_start(val_pool[n][:], vals[n * P : (n + 1) * P, :])
 
         ident = keep.tile([P, P], F32, name="ident")
         make_identity(nc, ident[:])
 
         halves = [slice(h * HALF, (h + 1) * HALF) for h in range(2)]
-        blocks = [slice(c * 8, (c + 1) * 8) for c in range(2)]
         list_halves = [slice(h * LIST_COLS // 2, (h + 1) * LIST_COLS // 2) for h in range(2)]
-
-        bias_g = keep.tile([P, I], F32, name="bias_g")
-        for h in range(2):
-            nc.vector.tensor_copy(bias_g[:, halves[h]], bias_pool[:].indirect(buckets[:, list_halves[h]]))
-
-        val_pool = {n: keep.tile([P, T], F32, name="val_pool%d" % n, align_bytes=64) for n in (0, 2, 3)}
-        val_rest = placed.tile([P, T - HEAD], F32, name="val_rest", offset=T // 2, align_bytes=64)
-        nc.sync.dma_start(val_rest[:], vals[P : 2 * P, HEAD:T])
-        nc.sync.dma_start(val_pool[0][:], vals[0:P, :])
-
-        k_codes = keep.tile([P, I], U32, name="k_codes", align_bytes=64)
 
         q_bf = keep.tile([P, Q, PACK], BF16, name="q_bf", align_bytes=64)
         nc.scalar.copy(q_bf[:], q_raw[:].rearrange("p j q -> p q j"))
         q_codes = keep.tile([P, Q], U32, name="q_codes", align_bytes=64)
-        q_scales = placed.tile([P, Q], U8, name="q_scales", offset=0, align_bytes=64)
+        q_scales = keep.tile([P, Q], U8, name="q_scales", align_bytes=64)
         nc.vector.quantize_mx(q_codes[:].bitcast(FP8X4), q_scales[:], q_bf[:].rearrange("p q j -> p (q j)"))
 
-        nc.scalar.copy(
-            q_raw[0:1].rearrange("p (h e) (g j) -> p h e g j", h=2, j=RUN // 2),
-            size_raw[:].rearrange("p (g h j e) -> p h e g j", h=2, j=RUN // 2, e=2),
-        )
+        nc.scalar.copy(q_raw[0:1], size_raw[:].rearrange("p (x t) -> p t x", t=PACK))
         nc.scalar.copy(q_raw[GATE_ROW : GATE_ROW + 1, 0, :], gate_raw[GATE_ROW:, :])
         rows_turned = psum.tile([P, PACK, P], F32, name="rows_turned", tag="mixed")
         for t in range(PACK):
@@ -104,6 +92,11 @@ def tile_attend_mixedbias_kernel(tc, query, keys_words, keys_scales, bias, gate,
         nc.scalar.copy(gate_col[:], rows_turned[:, 0, GATE_ROW : GATE_ROW + 1])
         nc.scalar.activation(rest_col[:], rows_turned[:, 0, GATE_ROW : GATE_ROW + 1], ACT.Copy, scale=-1.0, bias=1.0)
 
+        bias_g = keep.tile([P, I], F32, name="bias_g")
+        for h in range(2):
+            nc.scalar.activation(bias_g[:, halves[h]], bias_pool[:].indirect(buckets[:, list_halves[h]]), ACT.Copy)
+
+        k_codes = keep.tile([P, I], U32, name="k_codes", align_bytes=64)
         scores = []
         for h in range(2):
             nc.vector.tensor_copy(k_codes[:, halves[h]], word_pool[:].indirect(slots[:, list_halves[h]]))
@@ -118,83 +111,76 @@ def tile_attend_mixedbias_kernel(tc, query, keys_words, keys_scales, bias, gate,
                 stop=True,
             )
 
-        nc.sync.dma_start(val_pool[2][:], vals[2 * P : 3 * P, :])
-        val_bf = keep.tile([P, T], BF16, name="val_bf", align_bytes=64)
-        nc.scalar.copy(val_bf[:, 0:HEAD], val_head[:])
-        nc.sync.dma_start(val_pool[3][:], vals[3 * P : 4 * P, :])
-
-        def dealt(tile):
-            return tile[:].rearrange("p (h g r) -> p g h r", h=2, r=RUN)
+        cut = 16 * VECTOR_COLS
+        exp_and_first = keep.tile([P, I + (I - cut) // 2], F32, name="exp_and_first")
+        val_g = [exp_and_first[:, I - cut // 2 :].bitcast(BF16)]
+        val_g.extend(keep.tile([P, I], BF16, name="val_g%d" % n)[:] for n in range(1, E_TILES))
+        early_bf = placed.tile([P, 2 * I], BF16, name="early_bf", offset=POOL_BYTES + 2 * I, align_bytes=64)
+        late_bf = keep.tile([P, 2 * I], BF16, name="late_bf", align_bytes=64)
+        val_bf = [early_bf[:, 0:I], early_bf[:, I:], late_bf[:, 0:I], late_bf[:, I:]]
 
         def gather_values(n):
-            nc.vector.tensor_copy(dealt(val_g[n]), val_pool[n][:].indirect(slots[:]))
+            nc.vector.tensor_copy(val_g[n][:, 0:cut], val_pool[n][:].indirect(slots[:, 0:VECTOR_COLS]))
+            nc.scalar.activation(val_g[n][:, cut:I], val_pool[n][:].indirect(slots[:, VECTOR_COLS:LIST_COLS]), ACT.Copy)
 
-        def turn_values(n, val_g, grouped):
-            pairs = val_g[:].bitcast(F32)
+        def turn_values(n):
+            pairs = val_g[n].bitcast(F32)
             turned = turn.tile([P, 2, P], F32, name="turned")
-            for h in range(2):
-                nc.tensor.transpose(turned[:, h, :], pairs[:, h * P : (h + 1) * P], ident[:])
-            grouped_pairs = grouped.bitcast(F32).rearrange("p (x h) -> p x h", h=2)
+            for u in range(2):
+                nc.tensor.transpose(turned[:, u, :], pairs[:, u:HALF:2], ident[:])
+            grouped = val_bf[n].bitcast(F32).rearrange("p (x u) -> p x u", u=2)
             width = PIECE if n == E_TILES - 1 else P
             for first in range(0, P, width):
                 cols = slice(first, first + width)
-                nc.scalar.copy(grouped_pairs[:, cols, :], turned[:].rearrange("p h x -> p x h")[:, cols, :])
+                nc.scalar.copy(grouped[:, cols, :], turned[:].rearrange("p u x -> p x u")[:, cols, :])
 
-        late_bf = keep.tile([P, I], BF16, name="late_bf", align_bytes=64)
+        def paired(tile):
+            return tile[:].rearrange("p (u x e) -> p x u e", u=2, e=2)
 
         first_min = keep.tile([P, 1], F32, name="first_min")
         neg_max_r = keep.tile([P, 1], F32, name="neg_max_r")
         sum_r = keep.tile([P, 1], F32, name="sum_r")
+        sum_p = keep.tile([P, 1], F32, name="sum_p")
         biased = keep.tile([P, I], F32, name="biased")
         negated = keep.tile([P, I], F32, name="negated")
-        exp_r = keep.tile([P, I], F32, name="exp_r")
-        exp_p = keep.tile([P, I], F32, name="exp_p")
-        places_and_first = keep.tile([P, HALF + I], BF16, name="places_and_first")
-        w_places = places_and_first[:, 0:I].rearrange("p (t q) -> p t q", t=PACK)
-        val_g = [places_and_first[:, HALF:]]
-        val_g.extend(keep.tile([P, I], BF16, name="val_g%d" % n, tag=tag) for n, tag in ((1, "biased"), (2, "val_g2"), (3, "val_g3")))
-        neg_max_p = val_g[0][:].bitcast(F32)[:, 0:1]
-        sum_p = val_g[0][:].bitcast(F32)[:, HALF - 1 : HALF]
-        score_runs = [scores[c][:].rearrange("p (g h r) -> p g h r", h=2, r=RUN) for c in range(2)]
+        words = [slice(c * P // 2, (c + 1) * P // 2) for c in range(2)]
+        score_pairs = [scores[c][:].rearrange("p (x u e) -> p x u e", u=2, e=2) for c in range(2)]
         nc.vector.tensor_scalar(
-            dealt(negated)[:, blocks[0]], score_runs[0], -1.0, None, ALU.mult, ALU.min, accum_out=first_min[:]
+            paired(negated)[:, words[0]], score_pairs[0], -1.0, None, ALU.mult, ALU.min, accum_out=first_min[:]
         )
         for c in range(2):
             nc.vector.tensor_tensor(
-                dealt(biased)[:, blocks[c]],
-                score_runs[c],
-                bias_g[:, halves[c]].rearrange("p (g h r) -> p g h r", h=2, r=RUN),
+                paired(biased)[:, words[c]],
+                score_pairs[c],
+                bias_g[:, halves[c]].rearrange("p (x u e) -> p x u e", u=2, e=2),
                 ALU.add,
             )
         nc.vector.tensor_scalar(
-            dealt(negated)[:, blocks[1]], score_runs[1], -1.0, first_min[:], ALU.mult, ALU.min, accum_out=neg_max_r[:]
+            paired(negated)[:, words[1]], score_pairs[1], -1.0, first_min[:], ALU.mult, ALU.min, accum_out=neg_max_r[:]
         )
-        nc.vector.tensor_reduce(neg_max_p, biased[:], AXIS_X, ALU.max, negate=True)
+        exp_r = keep.tile([P, I], F32, name="exp_r")
+        neg_max_p = keep.tile([P, 1], F32, name="neg_max_p")
+        exp_p = exp_and_first[:, 0:I]
+        nc.vector.tensor_reduce(neg_max_p[:], biased[:], AXIS_X, ALU.max, negate=True)
         for exps, source, sign, neg_max, total in (
-            (exp_r, negated, -1.0, neg_max_r[:], sum_r[:]),
+            (exp_r, negated, -1.0, neg_max_r, sum_r),
             (exp_p, biased, 1.0, neg_max_p, sum_p),
         ):
             nc.scalar.activation(
-                exps[:].rearrange("p (h e x) -> p h e x", h=2, e=2),
-                source[:].rearrange("p (h x e) -> p h e x", h=2, e=2),
+                exps[:].rearrange("p (u e x) -> p u e x", u=2, e=2),
+                source[:].rearrange("p (u x e) -> p u e x", u=2, e=2),
                 ACT.Exp,
-                bias=neg_max,
+                bias=neg_max[:],
                 scale=sign,
-                accum_out=total,
+                accum_out=total[:],
             )
-
-
         part_r = keep.tile([P, I], F32, name="part_r")
         part_p = keep.tile([P, I], F32, name="part_p")
-        for name, part, exps, total, share in (("r", part_r, exp_r, sum_r[:], rest_col), ("p", part_p, exp_p, sum_p, gate_col)):
+        for name, part, exps, total, share in (("r", part_r, exp_r, sum_r, rest_col), ("p", part_p, exp_p, sum_p, gate_col)):
             inverse = keep.tile([P, 1], F32, name="inverse_" + name)
-            nc.vector.reciprocal(inverse[:], total)
+            nc.vector.reciprocal(inverse[:], total[:])
             nc.vector.tensor_scalar(part[:], exps[:], inverse[:], share[:], ALU.mult, ALU.mult)
-
-        rest_half = (T - HEAD) // 2
-        for first in range(0, T - HEAD, rest_half):
-            nc.scalar.copy(val_bf[:, HEAD + first : HEAD + first + rest_half], val_rest[:, first : first + rest_half])
-        nc.scalar.activation(dealt(val_g[1]), val_bf[:].indirect(slots[:]), ACT.Copy)
+        gather_values(0)
 
         mixed = psum.tile([P, PACK, P], F32, name="mixed")
         for k, part in enumerate((part_r, part_p)):
@@ -207,44 +193,32 @@ def tile_attend_mixedbias_kernel(tc, query, keys_words, keys_scales, bias, gate,
                     stop=(k == 1 and t == PACK - 1),
                     is_transpose=True,
                 )
-        early_bf = keep.tile([P, E_TILES * I], BF16, name="early_bf", tag="val_bf", align_bytes=64)
-        for c in range(2):
-            nc.vector.tensor_copy(dealt(val_g[0])[:, blocks[c]], val_pool[0][:].indirect(slots[:, list_halves[c]]))
-        for t in range(PACK):
-            if t == PACK // 2:
-                turn_values(1, val_g[1], early_bf[:, I : 2 * I])
-                turn_values(0, val_g[0], early_bf[:, 0:I])
-            nc.scalar.activation(w_places[:, t, :], mixed[:, t, :], ACT.Copy, scale=size_cols[:, t : t + 1])
-        nc.scalar.copy(
-            early_bf[:, 2 * I : 3 * I].rearrange("p (q t) -> p q t", t=PACK), w_places.rearrange("p t q -> p q t")
+        gather_values(1)
+        w_bf = placed.tile([P, Q, PACK], BF16, name="w_bf", offset=POOL_BYTES, align_bytes=64)
+        nc.vector.tensor_tensor(
+            w_bf[:],
+            mixed[:].rearrange("p t q -> p q t"),
+            size_cols[:].unsqueeze(1).to_broadcast([P, Q, PACK]),
+            ALU.mult,
         )
+        turn_values(0)
+        turn_values(1)
         gather_values(2)
-        first_codes = keep.tile([P, 2 * P], U32, name="first_codes", tag="val_pool2", align_bytes=64)
+        w_codes = placed.tile([P, Q], U32, name="w_codes", offset=2 * POOL_BYTES, align_bytes=64)
+        w_scales = keep.tile([P, Q], U8, name="w_scales", align_bytes=64)
+        nc.vector.quantize_mx(w_codes[:].bitcast(FP8X4), w_scales[:], w_bf[:].rearrange("p q t -> p (q t)"))
+        first_codes = placed.tile([P, 2 * P], U32, name="first_codes", offset=2 * POOL_BYTES + 4 * Q, align_bytes=64)
         first_scales = keep.tile([P, 2 * P], U8, name="first_scales", align_bytes=64)
-        nc.vector.quantize_mx(first_codes[:].bitcast(FP8X4), first_scales[:], early_bf[:, 0 : 2 * I])
-        turn_values(2, val_g[2], early_bf[:, 3 * I : 4 * I])
+        nc.vector.quantize_mx(first_codes[:].bitcast(FP8X4), first_scales[:], early_bf[:])
+        turn_values(2)
         gather_values(3)
-        turn_values(3, val_g[3], late_bf[:])
-
-        early_codes = keep.tile([P, 2 * P], U32, name="early_codes", tag="val_pool3", align_bytes=64)
-        early_scales = keep.tile([P, 2 * P], U8, name="early_scales", align_bytes=64)
-        nc.vector.quantize_mx(early_codes[:].bitcast(FP8X4), early_scales[:], early_bf[:, 2 * I : 4 * I])
-        late_codes = keep.tile([P, P], U32, name="late_codes", align_bytes=64)
-        late_scales = keep.tile([P, P], U8, name="late_scales", align_bytes=64)
-        pieces = [slice(c * PIECE, (c + 1) * PIECE) for c in range(LAST_PIECES)]
-        for c, cols in enumerate(pieces):
-            nc.vector.quantize_mx(
-                late_codes[:, cols].bitcast(FP8X4),
-                late_scales[:, cols],
-                late_bf[:, c * PIECE * PACK : (c + 1) * PIECE * PACK],
-            )
 
         def product(name, codes, scales, bank):
             acc = psum.tile([P, codes.shape[1]], F32, name=name + "_acc", tag=bank)
             nc.tensor.matmul_mx(
                 acc[:],
-                lhsT=early_codes[:, 0:Q].bitcast(FP8X4),
-                lhsT_scale=early_scales[:, 0:Q],
+                lhsT=w_codes[:].bitcast(FP8X4),
+                lhsT_scale=w_scales[:],
                 rhs=codes.bitcast(FP8X4),
                 rhs_scale=scales,
                 start=True,
@@ -252,13 +226,26 @@ def tile_attend_mixedbias_kernel(tc, query, keys_words, keys_scales, bias, gate,
             )
             return acc
 
-        early_out = keep.tile([P, 2 * P], F32, name="early_out")
-        mid_out = keep.tile([P, P], F32, name="mid_out")
-        late_out = keep.tile([P, P], F32, name="late_out")
         first_acc = product("first", first_codes[:], first_scales[:], "scores0")
-        mid_acc = product("mid", early_codes[:, P : 2 * P], early_scales[:, P : 2 * P], "mid_acc")
+        early_out = placed.tile([P, 2 * P], F32, name="early_out", offset=3 * POOL_BYTES, align_bytes=64)
         nc.scalar.copy(early_out[:], first_acc[:])
         nc.sync.dma_start(out[:, 0 : 2 * P], early_out[:])
+        mid_codes = placed.tile([P, P], U32, name="mid_codes", offset=3 * POOL_BYTES + 8 * P, align_bytes=64)
+        mid_scales = keep.tile([P, P], U8, name="mid_scales", align_bytes=64)
+        nc.vector.quantize_mx(mid_codes[:].bitcast(FP8X4), mid_scales[:], val_bf[2])
+        turn_values(3)
+        late_codes = keep.tile([P, P], U32, name="late_codes", align_bytes=64)
+        late_scales = keep.tile([P, P], U8, name="late_scales", align_bytes=64)
+        pieces = [slice(c * PIECE, (c + 1) * PIECE) for c in range(LAST_PIECES)]
+        for c, cols in enumerate(pieces):
+            nc.vector.quantize_mx(
+                late_codes[:, cols].bitcast(FP8X4),
+                late_scales[:, cols],
+                val_bf[3][:, c * PIECE * PACK : (c + 1) * PIECE * PACK],
+            )
+        mid_out = keep.tile([P, P], F32, name="mid_out")
+        late_out = keep.tile([P, P], F32, name="late_out")
+        mid_acc = product("mid", mid_codes[:], mid_scales[:], "scores1")
         nc.scalar.copy(mid_out[:], mid_acc[:])
         nc.sync.dma_start(out[:, 2 * P : 3 * P], mid_out[:])
         for c, bank in enumerate(("late_acc", "mixed")):

@@ -28,6 +28,7 @@ GATE_ROW = 32
 LAST_PIECES = 2
 PIECE = P // LAST_PIECES
 POOL_BYTES = 4 * T
+HEAD = 512
 VECTOR_COLS = 16
 
 
@@ -55,10 +56,10 @@ def tile_attend_mixedbias_kernel(tc, query, keys_words, keys_scales, bias, gate,
 
         nc.gpsimd.memset(byte_pool[0:ROW0, :].bitcast(I32), 0)
         nc.vector.memset(k_scales[:].bitcast(I32), 0)
-        nc.sync.dma_start(byte_pool[ROW0:P, :].bitcast(I32), keys_scales[0].bitcast(I32))
-        nc.scalar.dma_start(q_raw[:], query.rearrange("(p j) q -> p j q", j=PACK))
         nc.sync.dma_start(slots[:], offs)
         nc.scalar.dma_start(gate_raw[GATE_ROW:, :], gate.rearrange("q one -> one q"))
+        nc.sync.dma_start(byte_pool[ROW0:P, :].bitcast(I32), keys_scales[0].bitcast(I32))
+        nc.scalar.dma_start(q_raw[:], query.rearrange("(p j) q -> p j q", j=PACK))
         nc.sync.dma_start(buckets[:], offs2)
         nc.scalar.dma_start(size_raw[:], size)
         nc.sync.dma_start(word_pool[:].bitcast(I32), keys_words[0].rearrange("p n t -> p (n t)").bitcast(I32))
@@ -66,9 +67,11 @@ def tile_attend_mixedbias_kernel(tc, query, keys_words, keys_scales, bias, gate,
 
         row_scales = keep.tile([P, I], U8, name="row_scales")
         nc.vector.tensor_copy(row_scales[:], byte_pool[:].indirect(slots[:]))
+        nc.sync.dma_start(val_pool[0][:, 0:HEAD], vals[0:P, 0:HEAD])
         for r in range(4):
             nc.sync.dma_start(k_scales[r:P:32, :].bitcast(I32), row_scales[ROW0 + r : P : 4, :].bitcast(I32))
-        for n in range(E_TILES):
+        nc.sync.dma_start(val_pool[0][:, HEAD:T], vals[0:P, HEAD:T])
+        for n in range(1, E_TILES):
             nc.sync.dma_start(val_pool[n][:], vals[n * P : (n + 1) * P, :])
 
         ident = keep.tile([P, P], F32, name="ident")
@@ -93,8 +96,7 @@ def tile_attend_mixedbias_kernel(tc, query, keys_words, keys_scales, bias, gate,
         nc.scalar.activation(rest_col[:], rows_turned[:, 0, GATE_ROW : GATE_ROW + 1], ACT.Copy, scale=-1.0, bias=1.0)
 
         bias_g = keep.tile([P, I], F32, name="bias_g")
-        for h in range(2):
-            nc.scalar.activation(bias_g[:, halves[h]], bias_pool[:].indirect(buckets[:, list_halves[h]]), ACT.Copy)
+        nc.scalar.activation(bias_g[:, halves[0]], bias_pool[:].indirect(buckets[:, list_halves[0]]), ACT.Copy)
 
         k_codes = keep.tile([P, I], U32, name="k_codes", align_bytes=64)
         scores = []
@@ -113,11 +115,11 @@ def tile_attend_mixedbias_kernel(tc, query, keys_words, keys_scales, bias, gate,
 
         cut = 16 * VECTOR_COLS
         exp_and_first = keep.tile([P, I + (I - cut) // 2], F32, name="exp_and_first")
+        nc.vector.tensor_copy(bias_g[:, halves[1]], bias_pool[:].indirect(buckets[:, list_halves[1]]))
         val_g = [exp_and_first[:, I - cut // 2 :].bitcast(BF16)]
         val_g.extend(keep.tile([P, I], BF16, name="val_g%d" % n)[:] for n in range(1, E_TILES))
-        early_bf = placed.tile([P, 2 * I], BF16, name="early_bf", offset=POOL_BYTES + 2 * I, align_bytes=64)
-        late_bf = keep.tile([P, 2 * I], BF16, name="late_bf", align_bytes=64)
-        val_bf = [early_bf[:, 0:I], early_bf[:, I:], late_bf[:, 0:I], late_bf[:, I:]]
+        val_bf = [placed.tile([P, I], BF16, name="val_bf%d" % n, offset=(n + 1) * POOL_BYTES + 12 * Q, align_bytes=64)[:] for n in range(2)]
+        val_bf.extend(keep.tile([P, I], BF16, name="val_bf%d" % n, align_bytes=64)[:] for n in (2, 3))
 
         def gather_values(n):
             nc.vector.tensor_copy(val_g[n][:, 0:cut], val_pool[n][:].indirect(slots[:, 0:VECTOR_COLS]))
@@ -193,8 +195,8 @@ def tile_attend_mixedbias_kernel(tc, query, keys_words, keys_scales, bias, gate,
                     stop=(k == 1 and t == PACK - 1),
                     is_transpose=True,
                 )
-        gather_values(1)
-        w_bf = placed.tile([P, Q, PACK], BF16, name="w_bf", offset=POOL_BYTES, align_bytes=64)
+        nc.scalar.activation(val_g[1], val_pool[1][:].indirect(slots[:]), ACT.Copy)
+        w_bf = placed.tile([P, Q, PACK], BF16, name="w_bf", offset=0, align_bytes=64)
         nc.vector.tensor_tensor(
             w_bf[:],
             mixed[:].rearrange("p t q -> p q t"),
@@ -202,14 +204,15 @@ def tile_attend_mixedbias_kernel(tc, query, keys_words, keys_scales, bias, gate,
             ALU.mult,
         )
         turn_values(0)
-        turn_values(1)
         gather_values(2)
+        turn_values(1)
         w_codes = placed.tile([P, Q], U32, name="w_codes", offset=2 * POOL_BYTES, align_bytes=64)
         w_scales = keep.tile([P, Q], U8, name="w_scales", align_bytes=64)
         nc.vector.quantize_mx(w_codes[:].bitcast(FP8X4), w_scales[:], w_bf[:].rearrange("p q t -> p (q t)"))
         first_codes = placed.tile([P, 2 * P], U32, name="first_codes", offset=2 * POOL_BYTES + 4 * Q, align_bytes=64)
         first_scales = keep.tile([P, 2 * P], U8, name="first_scales", align_bytes=64)
-        nc.vector.quantize_mx(first_codes[:].bitcast(FP8X4), first_scales[:], early_bf[:])
+        for n in range(2):
+            nc.vector.quantize_mx(first_codes[:, n * P : (n + 1) * P].bitcast(FP8X4), first_scales[:, n * P : (n + 1) * P], val_bf[n])
         turn_values(2)
         gather_values(3)
 

@@ -24,7 +24,6 @@ HALF = I // 2
 LIST_COLS = I // 16
 SCALE_ROWS = D // 32
 ROW0 = P - SCALE_ROWS
-GATE_ROW = 32
 LAST_PIECES = 2
 PIECE = P // LAST_PIECES
 POOL_BYTES = 4 * T
@@ -38,7 +37,7 @@ def tile_attend_mixedbias_kernel(tc, query, keys_words, keys_scales, bias, gate,
         keep = ctx.enter_context(tc.tile_pool(name="keep", bufs=1))
         placed = ctx.enter_context(tc.tile_pool(name="placed", bufs=1))
         psum = ctx.enter_context(tc.psum_pool(name="psum", bufs=1))
-        turn = ctx.enter_context(tc.psum_pool(name="turn", bufs=2))
+        turn = ctx.enter_context(tc.psum_pool(name="turn", bufs=3))
 
         slots = keep.tile([P, LIST_COLS], U16, name="slots")
         buckets = keep.tile([P, LIST_COLS], U16, name="buckets")
@@ -47,21 +46,21 @@ def tile_attend_mixedbias_kernel(tc, query, keys_words, keys_scales, bias, gate,
         byte_pool = keep.tile([P, T], U8, name="byte_pool", align_bytes=64)
         k_scales = keep.tile([P, I], U8, name="k_scales", align_bytes=64)
         q_raw = keep.tile([P, PACK, Q], F32, name="q_raw")
-        gate_raw = keep.tile([GATE_ROW + 1, Q], F32, name="gate_raw")
         gate_col = keep.tile([P, 1], F32, name="gate_col")
         rest_col = keep.tile([P, 1], F32, name="rest_col")
-        size_raw = keep.tile([1, I], F32, name="size_raw")
+        rows = keep.tile([P, I + Q], F32, name="rows")
         size_cols = keep.tile([P, PACK], F32, name="size_cols")
         val_pool = [placed.tile([P, T], F32, name="val_pool%d" % n, offset=n * POOL_BYTES, align_bytes=64) for n in range(E_TILES)]
 
         nc.gpsimd.memset(byte_pool[0:ROW0, :].bitcast(I32), 0)
         nc.vector.memset(k_scales[:].bitcast(I32), 0)
+        nc.vector.memset(rows[0 : P - 1, :], 0.0)
         nc.sync.dma_start(slots[:], offs)
-        nc.scalar.dma_start(gate_raw[GATE_ROW:, :], gate.rearrange("q one -> one q"))
+        nc.scalar.dma_start(rows[P - 1 : P, I:], gate.rearrange("q one -> one q"))
         nc.sync.dma_start(byte_pool[ROW0:P, :].bitcast(I32), keys_scales[0].bitcast(I32))
         nc.scalar.dma_start(q_raw[:], query.rearrange("(p j) q -> p j q", j=PACK))
+        nc.sync.dma_start(rows[P - 1 : P, 0:I], size)
         nc.sync.dma_start(buckets[:], offs2)
-        nc.scalar.dma_start(size_raw[:], size)
         nc.sync.dma_start(word_pool[:].bitcast(I32), keys_words[0].rearrange("p n t -> p (n t)").bitcast(I32))
         nc.sync.dma_start(bias_pool[:], bias)
 
@@ -86,17 +85,18 @@ def tile_attend_mixedbias_kernel(tc, query, keys_words, keys_scales, bias, gate,
         q_scales = keep.tile([P, Q], U8, name="q_scales", align_bytes=64)
         nc.vector.quantize_mx(q_codes[:].bitcast(FP8X4), q_scales[:], q_bf[:].rearrange("p q j -> p (q j)"))
 
-        nc.scalar.copy(q_raw[0:1], size_raw[:].rearrange("p (x t) -> p t x", t=PACK))
-        nc.scalar.copy(q_raw[GATE_ROW : GATE_ROW + 1, 0, :], gate_raw[GATE_ROW:, :])
-        rows_turned = psum.tile([P, PACK, P], F32, name="rows_turned", tag="mixed")
+        size_turned = psum.tile([P, PACK, P], F32, name="size_turned", tag="mixed")
         for t in range(PACK):
-            nc.tensor.transpose(rows_turned[:, t, :], q_raw[:, t, :], ident[:])
-        nc.scalar.copy(size_cols[:], rows_turned[:, :, 0])
-        nc.scalar.copy(gate_col[:], rows_turned[:, 0, GATE_ROW : GATE_ROW + 1])
-        nc.scalar.activation(rest_col[:], rows_turned[:, 0, GATE_ROW : GATE_ROW + 1], ACT.Copy, scale=-1.0, bias=1.0)
+            nc.tensor.transpose(size_turned[:, t, :], rows[:, t:I:PACK], ident[:])
+        gate_turned = psum.tile([P, P], F32, name="gate_turned", tag="late_acc")
+        nc.tensor.transpose(gate_turned[:], rows[:, I:], ident[:])
+        nc.scalar.copy(size_cols[:], size_turned[:, :, P - 1])
+        nc.scalar.copy(gate_col[:], gate_turned[:, P - 1 : P])
+        nc.scalar.activation(rest_col[:], gate_turned[:, P - 1 : P], ACT.Copy, scale=-1.0, bias=1.0)
 
         bias_g = keep.tile([P, I], F32, name="bias_g")
-        nc.scalar.activation(bias_g[:, halves[0]], bias_pool[:].indirect(buckets[:, list_halves[0]]), ACT.Copy)
+        for h in range(2):
+            nc.scalar.activation(bias_g[:, halves[h]], bias_pool[:].indirect(buckets[:, list_halves[h]]), ACT.Copy)
 
         k_codes = keep.tile([P, I], U32, name="k_codes", align_bytes=64)
         scores = []
@@ -115,11 +115,10 @@ def tile_attend_mixedbias_kernel(tc, query, keys_words, keys_scales, bias, gate,
 
         cut = 16 * VECTOR_COLS
         exp_and_first = keep.tile([P, I + (I - cut) // 2], F32, name="exp_and_first")
-        nc.vector.tensor_copy(bias_g[:, halves[1]], bias_pool[:].indirect(buckets[:, list_halves[1]]))
         val_g = [exp_and_first[:, I - cut // 2 :].bitcast(BF16)]
         val_g.extend(keep.tile([P, I], BF16, name="val_g%d" % n)[:] for n in range(1, E_TILES))
-        val_bf = [placed.tile([P, I], BF16, name="val_bf%d" % n, offset=(n + 1) * POOL_BYTES + 12 * Q, align_bytes=64)[:] for n in range(2)]
-        val_bf.extend(keep.tile([P, I], BF16, name="val_bf%d" % n, align_bytes=64)[:] for n in (2, 3))
+        val_bf = [placed.tile([P, I], BF16, name="val_bf%d" % n, offset=(n + 1) * POOL_BYTES + 12 * Q, align_bytes=64)[:] for n in range(3)]
+        val_bf.append(keep.tile([P, I], BF16, name="val_bf3", align_bytes=64)[:])
 
         def gather_values(n):
             nc.vector.tensor_copy(val_g[n][:, 0:cut], val_pool[n][:].indirect(slots[:, 0:VECTOR_COLS]))
@@ -213,8 +212,8 @@ def tile_attend_mixedbias_kernel(tc, query, keys_words, keys_scales, bias, gate,
         first_scales = keep.tile([P, 2 * P], U8, name="first_scales", align_bytes=64)
         for n in range(2):
             nc.vector.quantize_mx(first_codes[:, n * P : (n + 1) * P].bitcast(FP8X4), first_scales[:, n * P : (n + 1) * P], val_bf[n])
-        turn_values(2)
         gather_values(3)
+        turn_values(2)
 
         def product(name, codes, scales, bank):
             acc = psum.tile([P, codes.shape[1]], F32, name=name + "_acc", tag=bank)
@@ -231,7 +230,7 @@ def tile_attend_mixedbias_kernel(tc, query, keys_words, keys_scales, bias, gate,
 
         first_acc = product("first", first_codes[:], first_scales[:], "scores0")
         early_out = placed.tile([P, 2 * P], F32, name="early_out", offset=3 * POOL_BYTES, align_bytes=64)
-        nc.scalar.copy(early_out[:], first_acc[:])
+        nc.vector.tensor_copy(early_out[:], first_acc[:])
         nc.sync.dma_start(out[:, 0 : 2 * P], early_out[:])
         mid_codes = placed.tile([P, P], U32, name="mid_codes", offset=3 * POOL_BYTES + 8 * P, align_bytes=64)
         mid_scales = keep.tile([P, P], U8, name="mid_scales", align_bytes=64)

@@ -52,9 +52,12 @@ def tile_attend_mixedbias_kernel(tc, query, keys_words, keys_scales, bias, gate,
         size_cols = keep.tile([P, PACK], F32, name="size_cols")
         val_pool = [placed.tile([P, T], F32, name="val_pool%d" % n, offset=n * POOL_BYTES, align_bytes=64) for n in range(E_TILES)]
 
-        nc.gpsimd.memset(byte_pool[0:ROW0, :].bitcast(I32), 0)
+        nc.vector.memset(byte_pool[0:ROW0, :].bitcast(I32), 0)
         nc.vector.memset(k_scales[:].bitcast(I32), 0)
         nc.vector.memset(rows[0 : P - 1, :], 0.0)
+        ident = keep.tile([P, P], F32, name="ident")
+        nc.vector.memset(ident[:], 0.0)
+        make_identity(nc, ident[:], nomemset=True)
         nc.sync.dma_start(slots[:], offs)
         nc.scalar.dma_start(rows[P - 1 : P, I:], gate.rearrange("q one -> one q"))
         nc.sync.dma_start(byte_pool[ROW0:P, :].bitcast(I32), keys_scales[0].bitcast(I32))
@@ -73,8 +76,6 @@ def tile_attend_mixedbias_kernel(tc, query, keys_words, keys_scales, bias, gate,
         for n in range(1, E_TILES):
             nc.sync.dma_start(val_pool[n][:], vals[n * P : (n + 1) * P, :])
 
-        ident = keep.tile([P, P], F32, name="ident")
-        make_identity(nc, ident[:])
 
         halves = [slice(h * HALF, (h + 1) * HALF) for h in range(2)]
         list_halves = [slice(h * LIST_COLS // 2, (h + 1) * LIST_COLS // 2) for h in range(2)]

@@ -27,7 +27,7 @@ ROW0 = P - SCALE_ROWS
 LAST_PIECES = 2
 PIECE = P // LAST_PIECES
 POOL_BYTES = 4 * T
-HEAD = 512
+HEAD = 256
 VECTOR_COLS = 16
 
 

@@ -41,20 +41,20 @@ def tile_attend_mixedbias_kernel(tc, query, keys_words, keys_scales, bias, gate,
 
         slots = keep.tile([P, LIST_COLS], U16, name="slots")
         buckets = keep.tile([P, LIST_COLS], U16, name="buckets")
-        bias_pool = keep.tile([P, U], F32, name="bias_pool", align_bytes=64)
-        word_pool = keep.tile([P, T], U32, name="word_pool", align_bytes=64)
-        byte_pool = keep.tile([P, T], U8, name="byte_pool", align_bytes=64)
-        k_scales = keep.tile([P, I], U8, name="k_scales", align_bytes=64)
-        q_raw = keep.tile([P, PACK, Q], F32, name="q_raw")
+        bias_pool = keep.tile([P, U], F32, name="bias_pool", align_bytes=256)
+        word_pool = keep.tile([P, T], U32, name="word_pool", align_bytes=256)
+        byte_pool = keep.tile([P, T], U8, name="byte_pool", align_bytes=256)
+        k_scales = keep.tile([P, I], U8, name="k_scales", align_bytes=256)
+        q_raw = keep.tile([P, PACK, Q], F32, name="q_raw", align_bytes=256)
         gate_col = keep.tile([P, 1], F32, name="gate_col")
         rest_col = keep.tile([P, 1], F32, name="rest_col")
         rows = keep.tile([P, I + Q], F32, name="rows")
         size_cols = keep.tile([P, PACK], F32, name="size_cols")
-        val_pool = [placed.tile([P, T], F32, name="val_pool%d" % n, offset=n * POOL_BYTES, align_bytes=64) for n in range(E_TILES)]
+        val_pool = [placed.tile([P, T], F32, name="val_pool%d" % n, offset=n * POOL_BYTES, align_bytes=256) for n in range(E_TILES)]
 
+        nc.vector.memset(rows[0 : P - 1, :], 0.0)
         nc.vector.memset(byte_pool[0:ROW0, :].bitcast(I32), 0)
         nc.vector.memset(k_scales[:].bitcast(I32), 0)
-        nc.vector.memset(rows[0 : P - 1, :], 0.0)
         ident = keep.tile([P, P], F32, name="ident")
         nc.vector.memset(ident[:], 0.0)
         make_identity(nc, ident[:], nomemset=True)
@@ -67,7 +67,7 @@ def tile_attend_mixedbias_kernel(tc, query, keys_words, keys_scales, bias, gate,
         nc.sync.dma_start(word_pool[:].bitcast(I32), keys_words[0].rearrange("p n t -> p (n t)").bitcast(I32))
         nc.sync.dma_start(bias_pool[:], bias)
 
-        row_scales = keep.tile([P, I], U8, name="row_scales")
+        row_scales = keep.tile([P, I], U8, name="row_scales", align_bytes=256)
         nc.vector.tensor_copy(row_scales[:], byte_pool[:].indirect(slots[:]))
         nc.sync.dma_start(val_pool[0][:, 0:HEAD], vals[0:P, 0:HEAD])
         for r in range(4):
@@ -246,8 +246,8 @@ def tile_attend_mixedbias_kernel(tc, query, keys_words, keys_scales, bias, gate,
                 late_scales[:, cols],
                 val_bf[3][:, c * PIECE * PACK : (c + 1) * PIECE * PACK],
             )
-        mid_out = keep.tile([P, P], F32, name="mid_out")
-        late_out = keep.tile([P, P], F32, name="late_out")
+        mid_out = keep.tile([P, P], F32, name="mid_out", align_bytes=256)
+        late_out = keep.tile([P, P], F32, name="late_out", align_bytes=256)
         mid_acc = product("mid", mid_codes[:], mid_scales[:], "scores1")
         nc.scalar.copy(mid_out[:], mid_acc[:])
         nc.sync.dma_start(out[:, 2 * P : 3 * P], mid_out[:])

from contextlib import ExitStack

import concourse.mybir as mybir
from concourse.masks import make_identity

D, T, I, Q, E, U = 512, 2048, 512, 128, 512, 512
FLOPS = 2 * Q * I * D + 2 * Q * I * E

F32 = mybir.dt.float32
BF16 = mybir.dt.bfloat16
I32 = mybir.dt.int32
U32 = mybir.dt.uint32
U16 = mybir.dt.uint16
U8 = mybir.dt.uint8
FP8X4 = mybir.dt.float8_e4m3fn_x4
ALU = mybir.AluOpType
ACT = mybir.ActivationFunctionType
AXIS_X = mybir.AxisListType.X

P = 128
PACK = 4
E_TILES = E // P
HALF = I // 2
LIST_COLS = I // 16
SCALE_ROWS = D // 32
ROW0 = P - SCALE_ROWS
LAST_PIECES = 2
PIECE = P // LAST_PIECES
POOL_BYTES = 4 * T
HEAD = 256
VECTOR_COLS = 16


def tile_attend_mixedbias_kernel(tc, query, keys_words, keys_scales, bias, gate, size, vals, offs, offs2, out):
    nc = tc.nc
    with ExitStack() as ctx:
        keep = ctx.enter_context(tc.tile_pool(name="keep", bufs=1))
        placed = ctx.enter_context(tc.tile_pool(name="placed", bufs=1))
        psum = ctx.enter_context(tc.psum_pool(name="psum", bufs=1))
        turn = ctx.enter_context(tc.psum_pool(name="turn", bufs=3))

        slots = keep.tile([P, LIST_COLS], U16, name="slots")
        buckets = keep.tile([P, LIST_COLS], U16, name="buckets")
        bias_pool = keep.tile([P, U], F32, name="bias_pool", align_bytes=256)
        word_pool = keep.tile([P, T], U32, name="word_pool", align_bytes=256)
        byte_pool = keep.tile([P, T], U8, name="byte_pool", align_bytes=256)
        k_scales = keep.tile([P, I], U8, name="k_scales", align_bytes=256)
        q_raw = keep.tile([P, PACK, Q], F32, name="q_raw", align_bytes=256)
        gate_col = keep.tile([P, 1], F32, name="gate_col")
        rest_col = keep.tile([P, 1], F32, name="rest_col")
        rows = keep.tile([P, I + Q], F32, name="rows")
        size_cols = keep.tile([P, PACK], F32, name="size_cols")
        val_pool = [placed.tile([P, T], F32, name="val_pool%d" % n, offset=n * POOL_BYTES, align_bytes=256) for n in range(E_TILES)]

        nc.vector.memset(rows[0 : P - 1, :], 0.0)
        nc.vector.memset(byte_pool[0:ROW0, :].bitcast(I32), 0)
        nc.vector.memset(k_scales[:].bitcast(I32), 0)
        ident = keep.tile([P, P], F32, name="ident")
        nc.vector.memset(ident[:], 0.0)
        make_identity(nc, ident[:], nomemset=True)
        nc.sync.dma_start(slots[:], offs)
        nc.scalar.dma_start(rows[P - 1 : P, I:], gate.rearrange("q one -> one q"))
        nc.sync.dma_start(byte_pool[ROW0:P, :].bitcast(I32), keys_scales[0].bitcast(I32))
        nc.scalar.dma_start(q_raw[:], query.rearrange("(p j) q -> p j q", j=PACK))
        nc.sync.dma_start(rows[P - 1 : P, 0:I], size)
        nc.sync.dma_start(buckets[:], offs2)
        nc.sync.dma_start(word_pool[:].bitcast(I32), keys_words[0].rearrange("p n t -> p (n t)").bitcast(I32))
        nc.sync.dma_start(bias_pool[:], bias)

        row_scales = keep.tile([P, I], U8, name="row_scales", align_bytes=256)
        nc.vector.tensor_copy(row_scales[:], byte_pool[:].indirect(slots[:]))
        nc.sync.dma_start(val_pool[0][:, 0:HEAD], vals[0:P, 0:HEAD])
        for r in range(4):
            nc.sync.dma_start(k_scales[r:P:32, :].bitcast(I32), row_scales[ROW0 + r : P : 4, :].bitcast(I32))
        nc.sync.dma_start(val_pool[0][:, HEAD:T], vals[0:P, HEAD:T])
        for n in range(1, E_TILES):
            nc.sync.dma_start(val_pool[n][:], vals[n * P : (n + 1) * P, :])


        halves = [slice(h * HALF, (h + 1) * HALF) for h in range(2)]
        list_halves = [slice(h * LIST_COLS // 2, (h + 1) * LIST_COLS // 2) for h in range(2)]

        q_bf = keep.tile([P, Q, PACK], BF16, name="q_bf", align_bytes=64)
        nc.scalar.copy(q_bf[:], q_raw[:].rearrange("p j q -> p q j"))
        q_codes = keep.tile([P, Q], U32, name="q_codes", align_bytes=64)
        q_scales = keep.tile([P, Q], U8, name="q_scales", align_bytes=64)
        nc.vector.quantize_mx(q_codes[:].bitcast(FP8X4), q_scales[:], q_bf[:].rearrange("p q j -> p (q j)"))

        size_turned = psum.tile([P, PACK, P], F32, name="size_turned", tag="mixed")
        for t in range(PACK):
            nc.tensor.transpose(size_turned[:, t, :], rows[:, t:I:PACK], ident[:])
        gate_turned = psum.tile([P, P], F32, name="gate_turned", tag="late_acc")
        nc.tensor.transpose(gate_turned[:], rows[:, I:], ident[:])
        nc.scalar.copy(size_cols[:], size_turned[:, :, P - 1])
        nc.scalar.copy(gate_col[:], gate_turned[:, P - 1 : P])
        nc.scalar.activation(rest_col[:], gate_turned[:, P - 1 : P], ACT.Copy, scale=-1.0, bias=1.0)

        bias_g = keep.tile([P, I], F32, name="bias_g")
        for h in range(2):
            nc.scalar.activation(bias_g[:, halves[h]], bias_pool[:].indirect(buckets[:, list_halves[h]]), ACT.Copy)

        k_codes = keep.tile([P, I], U32, name="k_codes", align_bytes=64)
        scores = []
        for h in range(2):
            nc.vector.tensor_copy(k_codes[:, halves[h]], word_pool[:].indirect(slots[:, list_halves[h]]))
            scores.append(psum.tile([P, HALF], F32, name="scores%d" % h))
            nc.tensor.matmul_mx(
                scores[h][:],
                lhsT=q_codes[:].bitcast(FP8X4),
                lhsT_scale=q_scales[:],
                rhs=k_codes[:, halves[h]].bitcast(FP8X4),
                rhs_scale=k_scales[:, halves[h]],
                start=True,
                stop=True,
            )

        cut = 16 * VECTOR_COLS
        exp_and_first = keep.tile([P, I + (I - cut) // 2], F32, name="exp_and_first")
        val_g = [exp_and_first[:, I - cut // 2 :].bitcast(BF16)]
        val_g.extend(keep.tile([P, I], BF16, name="val_g%d" % n)[:] for n in range(1, E_TILES))
        val_bf = [placed.tile([P, I], BF16, name="val_bf%d" % n, offset=(n + 1) * POOL_BYTES + 12 * Q, align_bytes=64)[:] for n in range(3)]
        val_bf.append(keep.tile([P, I], BF16, name="val_bf3", align_bytes=64)[:])

        def gather_values(n):
            nc.vector.tensor_copy(val_g[n][:, 0:cut], val_pool[n][:].indirect(slots[:, 0:VECTOR_COLS]))
            nc.scalar.activation(val_g[n][:, cut:I], val_pool[n][:].indirect(slots[:, VECTOR_COLS:LIST_COLS]), ACT.Copy)

        def turn_values(n):
            pairs = val_g[n].bitcast(F32)
            turned = turn.tile([P, 2, P], F32, name="turned")
            for u in range(2):
                nc.tensor.transpose(turned[:, u, :], pairs[:, u:HALF:2], ident[:])
            grouped = val_bf[n].bitcast(F32).rearrange("p (x u) -> p x u", u=2)
            width = PIECE if n == E_TILES - 1 else P
            for first in range(0, P, width):
                cols = slice(first, first + width)
                nc.scalar.copy(grouped[:, cols, :], turned[:].rearrange("p u x -> p x u")[:, cols, :])

        def paired(tile):
            return tile[:].rearrange("p (u x e) -> p x u e", u=2, e=2)

        first_min = keep.tile([P, 1], F32, name="first_min")
        neg_max_r = keep.tile([P, 1], F32, name="neg_max_r")
        sum_r = keep.tile([P, 1], F32, name="sum_r")
        sum_p = keep.tile([P, 1], F32, name="sum_p")
        biased = keep.tile([P, I], F32, name="biased")
        negated = keep.tile([P, I], F32, name="negated")
        words = [slice(c * P // 2, (c + 1) * P // 2) for c in range(2)]
        score_pairs = [scores[c][:].rearrange("p (x u e) -> p x u e", u=2, e=2) for c in range(2)]
        nc.vector.tensor_scalar(
            paired(negated)[:, words[0]], score_pairs[0], -1.0, None, ALU.mult, ALU.min, accum_out=first_min[:]
        )
        for c in range(2):
            nc.vector.tensor_tensor(
                paired(biased)[:, words[c]],
                score_pairs[c],
                bias_g[:, halves[c]].rearrange("p (x u e) -> p x u e", u=2, e=2),
                ALU.add,
            )
        nc.vector.tensor_scalar(
            paired(negated)[:, words[1]], score_pairs[1], -1.0, first_min[:], ALU.mult, ALU.min, accum_out=neg_max_r[:]
        )
        exp_r = keep.tile([P, I], F32, name="exp_r")
        neg_max_p = keep.tile([P, 1], F32, name="neg_max_p")
        exp_p = exp_and_first[:, 0:I]
        nc.vector.tensor_reduce(neg_max_p[:], biased[:], AXIS_X, ALU.max, negate=True)
        for exps, source, sign, neg_max, total in (
            (exp_r, negated, -1.0, neg_max_r, sum_r),
            (exp_p, biased, 1.0, neg_max_p, sum_p),
        ):
            nc.scalar.activation(
                exps[:].rearrange("p (u e x) -> p u e x", u=2, e=2),
                source[:].rearrange("p (u x e) -> p u e x", u=2, e=2),
                ACT.Exp,
                bias=neg_max[:],
                scale=sign,
                accum_out=total[:],
            )
        part_r = keep.tile([P, I], F32, name="part_r")
        part_p = keep.tile([P, I], F32, name="part_p")
        for name, part, exps, total, share in (("r", part_r, exp_r, sum_r, rest_col), ("p", part_p, exp_p, sum_p, gate_col)):
            inverse = keep.tile([P, 1], F32, name="inverse_" + name)
            nc.vector.reciprocal(inverse[:], total[:])
            nc.vector.tensor_scalar(part[:], exps[:], inverse[:], share[:], ALU.mult, ALU.mult)
        gather_values(0)

        mixed = psum.tile([P, PACK, P], F32, name="mixed")
        for k, part in enumerate((part_r, part_p)):
            for t in range(PACK):
                nc.tensor.matmul(
                    mixed[:, t, :],
                    part[:, t * P : (t + 1) * P],
                    ident[:],
                    start=(k == 0 and t == 0),
                    stop=(k == 1 and t == PACK - 1),
                    is_transpose=True,
                )
        nc.scalar.activation(val_g[1], val_pool[1][:].indirect(slots[:]), ACT.Copy)
        w_bf = placed.tile([P, Q, PACK], BF16, name="w_bf", offset=0, align_bytes=64)
        nc.vector.tensor_tensor(
            w_bf[:],
            mixed[:].rearrange("p t q -> p q t"),
            size_cols[:].unsqueeze(1).to_broadcast([P, Q, PACK]),
            ALU.mult,
        )
        turn_values(0)
        gather_values(2)
        turn_values(1)
        w_codes = placed.tile([P, Q], U32, name="w_codes", offset=2 * POOL_BYTES, align_bytes=64)
        w_scales = keep.tile([P, Q], U8, name="w_scales", align_bytes=64)
        nc.vector.quantize_mx(w_codes[:].bitcast(FP8X4), w_scales[:], w_bf[:].rearrange("p q t -> p (q t)"))
        first_codes = placed.tile([P, 2 * P], U32, name="first_codes", offset=2 * POOL_BYTES + 4 * Q, align_bytes=64)
        first_scales = keep.tile([P, 2 * P], U8, name="first_scales", align_bytes=64)
        for n in range(2):
            nc.vector.quantize_mx(first_codes[:, n * P : (n + 1) * P].bitcast(FP8X4), first_scales[:, n * P : (n + 1) * P], val_bf[n])
        gather_values(3)
        turn_values(2)

        def product(name, codes, scales, bank):
            acc = psum.tile([P, codes.shape[1]], F32, name=name + "_acc", tag=bank)
            nc.tensor.matmul_mx(
                acc[:],
                lhsT=w_codes[:].bitcast(FP8X4),
                lhsT_scale=w_scales[:],
                rhs=codes.bitcast(FP8X4),
                rhs_scale=scales,
                start=True,
                stop=True,
            )
            return acc

        first_acc = product("first", first_codes[:], first_scales[:], "scores0")
        early_out = placed.tile([P, 2 * P], F32, name="early_out", offset=3 * POOL_BYTES, align_bytes=64)
        nc.vector.tensor_copy(early_out[:], first_acc[:])
        nc.sync.dma_start(out[:, 0 : 2 * P], early_out[:])
        mid_codes = placed.tile([P, P], U32, name="mid_codes", offset=3 * POOL_BYTES + 8 * P, align_bytes=64)
        mid_scales = keep.tile([P, P], U8, name="mid_scales", align_bytes=64)
        nc.vector.quantize_mx(mid_codes[:].bitcast(FP8X4), mid_scales[:], val_bf[2])
        turn_values(3)
        late_codes = keep.tile([P, P], U32, name="late_codes", align_bytes=64)
        late_scales = keep.tile([P, P], U8, name="late_scales", align_bytes=64)
        pieces = [slice(c * PIECE, (c + 1) * PIECE) for c in range(LAST_PIECES)]
        for c, cols in enumerate(pieces):
            nc.vector.quantize_mx(
                late_codes[:, cols].bitcast(FP8X4),
                late_scales[:, cols],
                val_bf[3][:, c * PIECE * PACK : (c + 1) * PIECE * PACK],
            )
        mid_out = keep.tile([P, P], F32, name="mid_out", align_bytes=256)
        late_out = keep.tile([P, P], F32, name="late_out", align_bytes=256)
        mid_acc = product("mid", mid_codes[:], mid_scales[:], "scores1")
        nc.scalar.copy(mid_out[:], mid_acc[:])
        nc.sync.dma_start(out[:, 2 * P : 3 * P], mid_out[:])
        for c, bank in enumerate(("late_acc", "mixed")):
            acc = product("late%d" % c, late_codes[:, pieces[c]], late_scales[:, pieces[c]], bank)
            nc.vector.tensor_copy(late_out[:, pieces[c]], acc[:])
        nc.sync.dma_start(out[:, 3 * P : 4 * P], late_out[:])
